import numpy as np
import ml_dtypes


def mxq(x, axis, fmt="e4m3"):
    dtype, down = {"e4m3": (ml_dtypes.float8_e4m3fn, 7), "e5m2": (ml_dtypes.float8_e5m2, 14)}[fmt]
    v = np.moveaxis(np.asarray(x, np.float32).astype(ml_dtypes.bfloat16).astype(np.float64), axis, -1)
    blocks = v.reshape(v.shape[:-1] + (-1, 32))
    amax = np.abs(blocks).max(-1, keepdims=True)
    byte = np.maximum(np.where(amax > 0, np.frexp(amax)[1] - 1 + 127, 0) - down, 1)
    scale = np.exp2(byte - 127.0)
    codes = (blocks / scale).astype(np.float32).astype(dtype).astype(np.float64)
    return np.moveaxis((codes * scale).reshape(v.shape), -1, axis)


WIDE = False


def mx_kscale(k):
    if not WIDE:
        return np.ones(k)
    levels = np.array([10, -10, 5, -5, 0])
    if k % 512:
        return np.exp2(np.random.permutation(np.resize(levels, k // 32))).repeat(32)
    a = np.empty((k // 512, 16))
    for p in range(k // 512):
        a[p, :8] = np.random.permutation(np.resize(levels, 8))
        for g in range(8):
            far = levels[np.abs(levels - a[p, g]) >= 10]
            a[p, g + 8] = far[np.random.randint(len(far))]
    return np.exp2(a.ravel()).repeat(32)


def f64(x):
    return np.asarray(x).astype(np.float64)


def striped(idx):
    return np.tile(idx.reshape(-1, 16).T, (8, 1)).astype(np.uint16)


def unstriped(offs):
    return offs[:16].T.reshape(-1).astype(np.int64)


def pack_weight(w):
    k, n = w.shape
    w = f64(np.asarray(w, np.float32).astype(ml_dtypes.bfloat16)).reshape(k // 32, 32, n)
    amax = np.abs(w).max(1)
    byte = np.clip(np.where(amax > 0, np.frexp(amax)[1] - 1 + 127 - 7, 1), 1, 254)
    scaled = (w * np.exp2(127.0 - byte)[:, None, :]).reshape(k, n).astype(np.float32)
    words = np.ascontiguousarray(scaled.reshape(k // 512, 128, 4, n).transpose(0, 1, 3, 2)).astype(ml_dtypes.float8_e4m3fn).view(np.uint8)
    return words, np.ascontiguousarray(byte.astype(np.uint8).reshape(k // 512, 16, n))


def unpack_weight(words, scales):
    g, p, n, _ = words.shape
    vals = np.ascontiguousarray(words).view(ml_dtypes.float8_e4m3fn).astype(np.float64) * np.repeat(np.exp2(scales.astype(np.float64) - 127.0), 8, axis=1)[..., None]
    return vals.transpose(0, 1, 3, 2).reshape(g * 512, n)


K, T, S, H, V, W, G = 512, 1024, 512, 512, 512, 2048, 1024
P = 2 ** 7


def setup_inputs():
    n = np.random.standard_normal
    s = mx_kscale(K)[:, None]
    u = mx_kscale(H)
    packed_xT = pack_weight(n((K, T)) * s)
    packed_eT = pack_weight(n((K, W)) * s)
    packed_vT = pack_weight(n((H, G)) / np.sqrt(H) / u[:, None])
    return {
        "x_words": packed_xT[0],
        "x_scales": packed_xT[1],
        "e_words": packed_eT[0],
        "e_scales": packed_eT[1],
        "w1": (n((K, H)) / np.sqrt(K) / s * u).astype(np.float32),
        "w2": (n((K, H)) / np.sqrt(K) / s).astype(np.float32),
        "v_words": packed_vT[0],
        "v_scales": packed_vT[1],
        "phi": (np.tile(np.random.uniform(0.0, 1.0, G), (P, 1))).astype(np.float32),
        "lift": (n((S, V))).astype(np.float32),
        "offs": striped(np.random.permutation(T)[:S]),
        "coef": striped(np.random.permutation(W)[:S]),
        "pts": striped(np.random.permutation(G)[:V]),
    }


def reference(x_words, x_scales, e_words, e_scales, w1, w2, v_words, v_scales, phi, lift, offs, coef, pts):
    xq = unpack_weight(x_words, x_scales)[:, unstriped(offs)]
    y = mxq(f64(w1), 0, "e4m3").T @ xq
    e_coef = unpack_weight(e_words, e_scales)[:, unstriped(coef)]
    z = y * ((mxq(f64(w2), 0, "e4m3").T @ e_coef))
    v_pts = unpack_weight(v_words, v_scales)[:, unstriped(pts)]
    ss = mxq(z, 0, "e4m3").T @ v_pts
    return f64(lift) + ss * (f64(phi)[:1][:, unstriped(pts)])

@@ -1,0 +1,203 @@
+from contextlib import ExitStack
+
+import concourse.mybir as mybir
+from concourse.masks import make_identity
+
+K, T, S, H, V, W, G = 512, 1024, 512, 512, 512, 2048, 1024
+FLOPS = 2 * K * H * S * 2 + 2 * H * S * V
+
+F32 = mybir.dt.float32
+BF16 = mybir.dt.bfloat16
+I32 = mybir.dt.int32
+U32 = mybir.dt.uint32
+U16 = mybir.dt.uint16
+U8 = mybir.dt.uint8
+FP8X4 = mybir.dt.float8_e4m3fn_x4
+MULT = mybir.AluOpType.mult
+ADD = mybir.AluOpType.add
+
+P = 128
+PACK = 4
+CHUNKS = S // P
+
+
+def tile_picked_ymionet_val_p_kernel(
+    tc, x_words, x_scales, e_words, e_scales, w1, w2, v_words, v_scales, phi, lift, offs, coef, pts, out
+):
+    nc = tc.nc
+    with ExitStack() as ctx:
+        lists = ctx.enter_context(tc.tile_pool(name="lists", bufs=1))
+        sb = ctx.enter_context(tc.tile_pool(name="sb", bufs=1))
+        ps = ctx.enter_context(tc.psum_pool(name="ps", bufs=1))
+
+        def scale_table(name, width):
+            tile = sb.tile([P, width], U8, name=name, align_bytes=64)
+            nc.gpsimd.memset(tile[:].bitcast(I32), 0)
+            return tile
+
+        def load_scales(queue, tile, scales):
+            for q in range(4):
+                queue.dma_start(
+                    out=tile[32 * q : 32 * q + 4, :].bitcast(I32), in_=scales[0, 4 * q : 4 * q + 4, :].bitcast(I32)
+                )
+
+        def load_list(name, src):
+            tile = lists.tile([P, S // 16], U16, name=name)
+            nc.sync.dma_start(tile[:], src)
+            return tile
+
+        def load_words(name, words, width):
+            tile = sb.tile([P, width], I32, name=name, align_bytes=64)
+            nc.sync.dma_start(out=tile[:], in_=words[0].rearrange("p n t -> p (n t)").bitcast(I32))
+            return tile
+
+        def load_weight(name, w, c0, c1):
+            tile = sb.tile([P, PACK, c1 - c0], F32, name=name, tag=name)
+            nc.sync.dma_start(out=tile[:], in_=w.rearrange("(p j) c -> p j c", j=PACK)[:, :, c0:c1])
+            return tile
+
+        def cast_weight(grouped, raw, c0, c1):
+            nc.scalar.copy(
+                out=grouped[:].rearrange("p (t m j) -> p m j t", t=PACK, j=PACK)[:, c0 // PACK : c1 // PACK],
+                in_=raw[:].rearrange("p j (m t) -> p m j t", t=PACK),
+            )
+
+        def quantize(name, grouped):
+            codes = sb.tile([P, H], U32, name=name + "_codes", align_bytes=64)
+            scales = sb.tile([P, H], U8, name=name + "_scales", align_bytes=64)
+            nc.vector.quantize_mx(out=codes[:].bitcast(FP8X4), scales=scales[:], in_=grouped[:])
+            return codes, scales
+
+        xs_tab = scale_table("xs_tab", T)
+        es_tab = scale_table("es_tab", W)
+        vs_tab = scale_table("vs_tab", G)
+
+        ident = sb.tile([P, P], F32, name="ident")
+        make_identity(nc, ident[:])
+
+        offs_sb = load_list("offs_sb", offs)
+        load_scales(nc.sync, xs_tab, x_scales)
+        phi_cols = sb.tile([P, G // P], F32, name="phi_cols")
+        nc.sync.dma_start(out=phi_cols[:], in_=phi[0].rearrange("(p c) -> p c", p=P))
+        xw_tab = load_words("xw_tab", x_words, T)
+        w1_lo = load_weight("w1_lo", w1, 0, H // 2)
+        coef_sb = load_list("coef_sb", coef)
+        load_scales(nc.sync, es_tab, e_scales)
+        pts_sb = load_list("pts_sb", pts)
+        w1_hi = load_weight("w1_hi", w1, H // 2, H)
+        w2_lo = load_weight("w2_lo", w2, 0, H // 2)
+        load_scales(nc.sync, vs_tab, v_scales)
+        w2_hi = load_weight("w2_hi", w2, H // 2, H)
+        ew_tab = load_words("ew_tab", e_words, W)
+        vw_tab = load_words("vw_tab", v_words, G)
+        lift_sb = []
+        for h in range(2):
+            tile = sb.tile([P, 2, V], F32, name="lift%d" % h)
+            nc.sync.dma_start(out=tile[:], in_=lift[2 * P * h : 2 * P * (h + 1), :].rearrange("(c p) v -> p c v", p=P))
+            lift_sb.append(tile)
+
+        xs = sb.tile([P, S], U8, name="xs", align_bytes=64)
+        es = sb.tile([P, S], U8, name="es", align_bytes=64)
+        vs = sb.tile([P, V], U8, name="vs", align_bytes=64)
+        xw = sb.tile([P, S], U32, name="xw", align_bytes=64)
+        ew = sb.tile([P, S], U32, name="ew", align_bytes=64)
+        vw = sb.tile([P, V], U32, name="vw", align_bytes=64)
+        phi_pts = sb.tile([P, V], F32, name="phi_pts")
+        w1_bf = sb.tile([P, H * PACK], BF16, name="w1_bf", align_bytes=64)
+        w2_bf = sb.tile([P, H * PACK], BF16, name="w2_bf", align_bytes=64)
+
+        phi_tab = sb.tile([P, G], F32, name="phi_tab")
+        for h in range(2):
+            bank = ps.tile([P, 4, P], F32, name="phi_bank%d" % h, tag="b%d" % h)
+            for c in range(4):
+                nc.tensor.transpose(bank[:, c, :], phi_cols[:, 4 * h + c : 4 * h + c + 1].to_broadcast([P, P]), ident[:])
+            nc.scalar.copy(
+                out=phi_tab[:].rearrange("m (p c) -> m p c", p=P)[:, :, 4 * h : 4 * h + 4],
+                in_=bank[:].rearrange("m c p -> m p c"),
+            )
+
+        nc.vector.tensor_copy(xs[:], xs_tab[:].indirect(offs_sb[:]))
+        nc.vector.tensor_copy(xw[:], xw_tab[:].bitcast(U32).indirect(offs_sb[:]))
+        nc.vector.tensor_copy(es[:], es_tab[:].indirect(coef_sb[:]))
+        nc.vector.tensor_copy(phi_pts[:], phi_tab[:].indirect(pts_sb[:]))
+        cast_weight(w1_bf, w1_lo, 0, H // 2)
+        cast_weight(w1_bf, w1_hi, H // 2, H)
+        w1_codes, w1_scales = quantize("w1", w1_bf)
+        nc.vector.tensor_copy(vs[:], vs_tab[:].indirect(pts_sb[:]))
+        cast_weight(w2_bf, w2_lo, 0, H // 2)
+        cast_weight(w2_bf, w2_hi, H // 2, H)
+
+        def first_product(bank, codes, scales, words, word_scales, c):
+            cols = slice(c * P, (c + 1) * P)
+            for j in range(PACK):
+                hid = slice(j * P, (j + 1) * P)
+                nc.tensor.matmul_mx(
+                    out=bank[:, j, :],
+                    lhsT=codes[:, hid].bitcast(FP8X4),
+                    lhsT_scale=scales[:, hid],
+                    rhs=words[:, cols].bitcast(FP8X4),
+                    rhs_scale=word_scales[:, cols],
+                    start=True,
+                    stop=True,
+                )
+
+        y_sb = sb.tile([P, CHUNKS, P, PACK], F32, name="y_sb", tag="w2_hi")
+        for c in range(CHUNKS):
+            bank = ps.tile([P, PACK, P], F32, name="ya%d" % c, tag="a%d" % c)
+            first_product(bank, w1_codes, w1_scales, xw, xs, c)
+            nc.scalar.copy(out=y_sb[:, c], in_=bank[:].rearrange("p j t -> p t j"))
+
+        w2_codes, w2_scales = quantize("w2", w2_bf)
+        for h in range(2):
+            nc.vector.tensor_copy(
+                ew[:, 256 * h : 256 * (h + 1)], ew_tab[:].bitcast(U32).indirect(coef_sb[:, 16 * h : 16 * (h + 1)])
+            )
+        e_banks = []
+        for c in range(CHUNKS):
+            bank = ps.tile([P, PACK, P], F32, name="yb%d" % c, tag="b%d" % c)
+            first_product(bank, w2_codes, w2_scales, ew, es, c)
+            e_banks.append(bank)
+        nc.vector.tensor_copy(vw[:], vw_tab[:].bitcast(U32).indirect(pts_sb[:]))
+
+        z_bf = [sb.tile([P, P, PACK], BF16, name="z_bf%d" % c, align_bytes=64) for c in range(CHUNKS)]
+        z_codes = [sb.tile([P, P], U32, name="z_codes%d" % c, align_bytes=64) for c in range(CHUNKS)]
+        z_scales = [sb.tile([P, P], U8, name="z_scales%d" % c, align_bytes=64) for c in range(CHUNKS)]
+        scaled = [sb.tile([P, V], F32, name="scaled%d" % c) for c in range(CHUNKS)]
+        result = [sb.tile([P, V], F32, name="result%d" % c) for c in range(CHUNKS)]
+        ss = [None] * CHUNKS
+
+        def make_z(c):
+            nc.vector.tensor_tensor(z_bf[c][:], e_banks[c][:].rearrange("p j t -> p t j"), y_sb[:, c], MULT)
+
+        def second_product(c):
+            nc.vector.quantize_mx(
+                out=z_codes[c][:].bitcast(FP8X4), scales=z_scales[c][:], in_=z_bf[c][:].rearrange("p t j -> p (t j)")
+            )
+            ss[c] = ps.tile([P, V], F32, name="ss%d" % c, tag="a%d" % c)
+            nc.tensor.matmul_mx(
+                out=ss[c][:],
+                lhsT=z_codes[c][:].bitcast(FP8X4),
+                lhsT_scale=z_scales[c][:],
+                rhs=vw[:].bitcast(FP8X4),
+                rhs_scale=vs[:],
+                start=True,
+                stop=True,
+            )
+
+        def scale(c):
+            nc.vector.tensor_tensor(scaled[c][:], ss[c][:], phi_pts[:], MULT)
+
+        def finish(c):
+            nc.vector.tensor_tensor(result[c][:], scaled[c][:], lift_sb[c // 2][:, c % 2, :], ADD)
+            nc.sync.dma_start(out=out[c * P : (c + 1) * P, :], in_=result[c][:])
+
+        make_z(0)
+        for c in range(CHUNKS):
+            if c + 1 < CHUNKS:
+                make_z(c + 1)
+            second_product(c)
+        scale(0)
+        for c in range(CHUNKS):
+            if c + 1 < CHUNKS:
+                scale(c + 1)
+            finish(c)

@@ -28,6 +28,7 @@ def tile_picked_ymionet_val_p_kernel(
     with ExitStack() as ctx:
         lists = ctx.enter_context(tc.tile_pool(name="lists", bufs=1))
         sb = ctx.enter_context(tc.tile_pool(name="sb", bufs=1))
+        reuse = ctx.enter_context(tc.tile_pool(name="reuse", bufs=1))
         ps = ctx.enter_context(tc.psum_pool(name="ps", bufs=1))
 
         def scale_table(name, width):
@@ -35,9 +36,9 @@ def tile_picked_ymionet_val_p_kernel(
             nc.gpsimd.memset(tile[:].bitcast(I32), 0)
             return tile
 
-        def load_scales(queue, tile, scales):
+        def load_scales(queues, tile, scales):
             for q in range(4):
-                queue.dma_start(
+                queues[q].dma_start(
                     out=tile[32 * q : 32 * q + 4, :].bitcast(I32), in_=scales[0, 4 * q : 4 * q + 4, :].bitcast(I32)
                 )
 
@@ -76,17 +77,17 @@ def tile_picked_ymionet_val_p_kernel(
         make_identity(nc, ident[:])
 
         offs_sb = load_list("offs_sb", offs)
-        load_scales(nc.sync, xs_tab, x_scales)
-        phi_cols = sb.tile([P, G // P], F32, name="phi_cols")
-        nc.sync.dma_start(out=phi_cols[:], in_=phi[0].rearrange("(p c) -> p c", p=P))
+        load_scales([nc.scalar, nc.scalar, nc.sync, nc.sync], xs_tab, x_scales)
+        phi_cols = reuse.tile([P, G // P], F32, name="phi_cols", align_bytes=64, offset=0)
+        nc.scalar.dma_start(out=phi_cols[:], in_=phi[0].rearrange("(p c) -> p c", p=P))
         xw_tab = load_words("xw_tab", x_words, T)
         w1_lo = load_weight("w1_lo", w1, 0, H // 2)
         coef_sb = load_list("coef_sb", coef)
-        load_scales(nc.sync, es_tab, e_scales)
+        load_scales([nc.sync] * 4, es_tab, e_scales)
         pts_sb = load_list("pts_sb", pts)
         w1_hi = load_weight("w1_hi", w1, H // 2, H)
         w2_lo = load_weight("w2_lo", w2, 0, H // 2)
-        load_scales(nc.sync, vs_tab, v_scales)
+        load_scales([nc.sync] * 4, vs_tab, v_scales)
         w2_hi = load_weight("w2_hi", w2, H // 2, H)
         ew_tab = load_words("ew_tab", e_words, W)
         vw_tab = load_words("vw_tab", v_words, G)
@@ -94,17 +95,12 @@ def tile_picked_ymionet_val_p_kernel(
         for h in range(2):
             tile = sb.tile([P, 2, V], F32, name="lift%d" % h)
             nc.sync.dma_start(out=tile[:], in_=lift[2 * P * h : 2 * P * (h + 1), :].rearrange("(c p) v -> p c v", p=P))
-            lift_sb.append(tile)
+            lift_sb.extend([tile[:, c, :] for c in range(2)])
 
         xs = sb.tile([P, S], U8, name="xs", align_bytes=64)
         es = sb.tile([P, S], U8, name="es", align_bytes=64)
-        vs = sb.tile([P, V], U8, name="vs", align_bytes=64)
         xw = sb.tile([P, S], U32, name="xw", align_bytes=64)
-        ew = sb.tile([P, S], U32, name="ew", align_bytes=64)
-        vw = sb.tile([P, V], U32, name="vw", align_bytes=64)
         phi_pts = sb.tile([P, V], F32, name="phi_pts")
-        w1_bf = sb.tile([P, H * PACK], BF16, name="w1_bf", align_bytes=64)
-        w2_bf = sb.tile([P, H * PACK], BF16, name="w2_bf", align_bytes=64)
 
         phi_tab = sb.tile([P, G], F32, name="phi_tab")
         for h in range(2):
@@ -120,10 +116,13 @@ def tile_picked_ymionet_val_p_kernel(
         nc.vector.tensor_copy(xw[:], xw_tab[:].bitcast(U32).indirect(offs_sb[:]))
         nc.vector.tensor_copy(es[:], es_tab[:].indirect(coef_sb[:]))
         nc.vector.tensor_copy(phi_pts[:], phi_tab[:].indirect(pts_sb[:]))
+        w1_bf = reuse.tile([P, H * PACK], BF16, name="w1_bf", align_bytes=64, offset=0)
         cast_weight(w1_bf, w1_lo, 0, H // 2)
         cast_weight(w1_bf, w1_hi, H // 2, H)
         w1_codes, w1_scales = quantize("w1", w1_bf)
+        vs = reuse.tile([P, V], U8, name="vs", align_bytes=64, offset=0)
         nc.vector.tensor_copy(vs[:], vs_tab[:].indirect(pts_sb[:]))
+        w2_bf = reuse.tile([P, H * PACK], BF16, name="w2_bf", align_bytes=64, offset=4096)
         cast_weight(w2_bf, w2_lo, 0, H // 2)
         cast_weight(w2_bf, w2_hi, H // 2, H)
 
@@ -148,6 +147,8 @@ def tile_picked_ymionet_val_p_kernel(
             nc.scalar.copy(out=y_sb[:, c], in_=bank[:].rearrange("p j t -> p t j"))
 
         w2_codes, w2_scales = quantize("w2", w2_bf)
+        ew = reuse.tile([P, S], U32, name="ew", align_bytes=64, offset=4096)
+        vw = reuse.tile([P, V], U32, name="vw", align_bytes=64, offset=6144)
         for h in range(2):
             nc.vector.tensor_copy(
                 ew[:, 256 * h : 256 * (h + 1)], ew_tab[:].bitcast(U32).indirect(coef_sb[:, 16 * h : 16 * (h + 1)])
@@ -169,10 +170,12 @@ def tile_picked_ymionet_val_p_kernel(
         def make_z(c):
             nc.vector.tensor_tensor(z_bf[c][:], e_banks[c][:].rearrange("p j t -> p t j"), y_sb[:, c], MULT)
 
-        def second_product(c):
+        def quantize_z(c):
             nc.vector.quantize_mx(
                 out=z_codes[c][:].bitcast(FP8X4), scales=z_scales[c][:], in_=z_bf[c][:].rearrange("p t j -> p (t j)")
             )
+
+        def product_plain(c):
             ss[c] = ps.tile([P, V], F32, name="ss%d" % c, tag="a%d" % c)
             nc.tensor.matmul_mx(
                 out=ss[c][:],
@@ -187,17 +190,19 @@ def tile_picked_ymionet_val_p_kernel(
         def scale(c):
             nc.vector.tensor_tensor(scaled[c][:], ss[c][:], phi_pts[:], MULT)
 
-        def finish(c):
-            nc.vector.tensor_tensor(result[c][:], scaled[c][:], lift_sb[c // 2][:, c % 2, :], ADD)
+        def finish(engine, c):
+            engine.tensor_tensor(result[c][:], scaled[c][:], lift_sb[c], ADD)
             nc.sync.dma_start(out=out[c * P : (c + 1) * P, :], in_=result[c][:])
 
         make_z(0)
         for c in range(CHUNKS):
             if c + 1 < CHUNKS:
                 make_z(c + 1)
-            second_product(c)
+            quantize_z(c)
+            product_plain(c)
         scale(0)
-        for c in range(CHUNKS):
-            if c + 1 < CHUNKS:
-                scale(c + 1)
-            finish(c)
+        finish(nc.gpsimd, 0)
+        for c in range(1, CHUNKS):
+            scale(c)
+        for c in range(1, CHUNKS):
+            finish(nc.vector, c)

@@ -19,6 +19,7 @@ ADD = mybir.AluOpType.add
 P = 128
 PACK = 4
 CHUNKS = S // P
+X_ROW, E_ROW, V_ROW = 0, 4, 8
 
 
 def tile_picked_ymionet_val_p_kernel(
@@ -36,10 +37,10 @@ def tile_picked_ymionet_val_p_kernel(
             nc.gpsimd.memset(tile[:].bitcast(I32), 0)
             return tile
 
-        def load_scales(queues, tile, scales):
-            for q in range(4):
-                queues[q].dma_start(
-                    out=tile[32 * q : 32 * q + 4, :].bitcast(I32), in_=scales[0, 4 * q : 4 * q + 4, :].bitcast(I32)
+        def load_scales(queues, tile, scales, row):
+            for r in range(4):
+                queues[r].dma_start(
+                    out=tile[row + r : P : 32, :].bitcast(I32), in_=scales[0, r:16:4, :].bitcast(I32)
                 )
 
         def load_list(name, src):
@@ -77,17 +78,17 @@ def tile_picked_ymionet_val_p_kernel(
         make_identity(nc, ident[:])
 
         offs_sb = load_list("offs_sb", offs)
-        load_scales([nc.scalar, nc.scalar, nc.sync, nc.sync], xs_tab, x_scales)
+        load_scales([nc.scalar, nc.scalar, nc.sync, nc.sync], xs_tab, x_scales, X_ROW)
         phi_cols = reuse.tile([P, G // P], F32, name="phi_cols", align_bytes=64, offset=0)
         nc.scalar.dma_start(out=phi_cols[:], in_=phi[0].rearrange("(p c) -> p c", p=P))
         xw_tab = load_words("xw_tab", x_words, T)
         w1_lo = load_weight("w1_lo", w1, 0, H // 2)
         coef_sb = load_list("coef_sb", coef)
-        load_scales([nc.sync] * 4, es_tab, e_scales)
+        load_scales([nc.sync] * 4, es_tab, e_scales, E_ROW)
         pts_sb = load_list("pts_sb", pts)
         w1_hi = load_weight("w1_hi", w1, H // 2, H)
         w2_lo = load_weight("w2_lo", w2, 0, H // 2)
-        load_scales([nc.sync] * 4, vs_tab, v_scales)
+        load_scales([nc.sync] * 4, vs_tab, v_scales, V_ROW)
         w2_hi = load_weight("w2_hi", w2, H // 2, H)
         ew_tab = load_words("ew_tab", e_words, W)
         vw_tab = load_words("vw_tab", v_words, G)
@@ -126,7 +127,7 @@ def tile_picked_ymionet_val_p_kernel(
         cast_weight(w2_bf, w2_lo, 0, H // 2)
         cast_weight(w2_bf, w2_hi, H // 2, H)
 
-        def first_product(bank, codes, scales, words, word_scales, c):
+        def first_product(bank, codes, scales, words, word_scales, row, c):
             cols = slice(c * P, (c + 1) * P)
             for j in range(PACK):
                 hid = slice(j * P, (j + 1) * P)
@@ -135,7 +136,7 @@ def tile_picked_ymionet_val_p_kernel(
                     lhsT=codes[:, hid].bitcast(FP8X4),
                     lhsT_scale=scales[:, hid],
                     rhs=words[:, cols].bitcast(FP8X4),
-                    rhs_scale=word_scales[:, cols],
+                    rhs_scale=word_scales[row:P, cols],
                     start=True,
                     stop=True,
                 )
@@ -143,7 +144,7 @@ def tile_picked_ymionet_val_p_kernel(
         y_sb = sb.tile([P, CHUNKS, P, PACK], F32, name="y_sb", tag="w2_hi")
         for c in range(CHUNKS):
             bank = ps.tile([P, PACK, P], F32, name="ya%d" % c, tag="a%d" % c)
-            first_product(bank, w1_codes, w1_scales, xw, xs, c)
+            first_product(bank, w1_codes, w1_scales, xw, xs, X_ROW, c)
             nc.scalar.copy(out=y_sb[:, c], in_=bank[:].rearrange("p j t -> p t j"))
 
         w2_codes, w2_scales = quantize("w2", w2_bf)
@@ -156,7 +157,7 @@ def tile_picked_ymionet_val_p_kernel(
         e_banks = []
         for c in range(CHUNKS):
             bank = ps.tile([P, PACK, P], F32, name="yb%d" % c, tag="b%d" % c)
-            first_product(bank, w2_codes, w2_scales, ew, es, c)
+            first_product(bank, w2_codes, w2_scales, ew, es, E_ROW, c)
             e_banks.append(bank)
         nc.vector.tensor_copy(vw[:], vw_tab[:].bitcast(U32).indirect(pts_sb[:]))
 
@@ -182,7 +183,7 @@ def tile_picked_ymionet_val_p_kernel(
                 lhsT=z_codes[c][:].bitcast(FP8X4),
                 lhsT_scale=z_scales[c][:],
                 rhs=vw[:].bitcast(FP8X4),
-                rhs_scale=vs[:],
+                rhs_scale=vs[V_ROW:P, :],
                 start=True,
                 stop=True,
             )

@@ -15,6 +15,7 @@ U8 = mybir.dt.uint8
 FP8X4 = mybir.dt.float8_e4m3fn_x4
 MULT = mybir.AluOpType.mult
 ADD = mybir.AluOpType.add
+COPY = mybir.ActivationFunctionType.Copy
 
 P = 128
 PACK = 4
@@ -53,8 +54,8 @@ def tile_picked_ymionet_val_p_kernel(
             nc.sync.dma_start(out=tile[:], in_=words[0].rearrange("p n t -> p (n t)").bitcast(I32))
             return tile
 
-        def load_weight(name, w, c0, c1):
-            tile = sb.tile([P, PACK, c1 - c0], F32, name=name, tag=name)
+        def load_weight(name, w, c0, c1, offset):
+            tile = reuse.tile([P, PACK, c1 - c0], F32, name=name, align_bytes=64, offset=offset)
             nc.sync.dma_start(out=tile[:], in_=w.rearrange("(p j) c -> p j c", j=PACK)[:, :, c0:c1])
             return tile
 
@@ -82,14 +83,14 @@ def tile_picked_ymionet_val_p_kernel(
         phi_cols = reuse.tile([P, G // P], F32, name="phi_cols", align_bytes=64, offset=0)
         nc.scalar.dma_start(out=phi_cols[:], in_=phi[0].rearrange("(p c) -> p c", p=P))
         xw_tab = load_words("xw_tab", x_words, T)
-        w1_lo = load_weight("w1_lo", w1, 0, H // 2)
+        w1_lo = load_weight("w1_lo", w1, 0, H // 2, 28672)
         coef_sb = load_list("coef_sb", coef)
         load_scales([nc.sync] * 4, es_tab, e_scales, E_ROW)
         pts_sb = load_list("pts_sb", pts)
-        w1_hi = load_weight("w1_hi", w1, H // 2, H)
-        w2_lo = load_weight("w2_lo", w2, 0, H // 2)
+        w1_hi = load_weight("w1_hi", w1, H // 2, H, 32768)
+        w2_lo = load_weight("w2_lo", w2, 0, H // 2, 36864)
         load_scales([nc.sync] * 4, vs_tab, v_scales, V_ROW)
-        w2_hi = load_weight("w2_hi", w2, H // 2, H)
+        w2_hi = load_weight("w2_hi", w2, H // 2, H, 12288)
         ew_tab = load_words("ew_tab", e_words, W)
         vw_tab = load_words("vw_tab", v_words, G)
         lift_sb = []
@@ -135,33 +136,42 @@ def tile_picked_ymionet_val_p_kernel(
                     out=bank[:, j, :],
                     lhsT=codes[:, hid].bitcast(FP8X4),
                     lhsT_scale=scales[:, hid],
-                    rhs=words[:, cols].bitcast(FP8X4),
+                    rhs=words.bitcast(FP8X4),
                     rhs_scale=word_scales[row:P, cols],
                     start=True,
                     stop=True,
                 )
 
-        y_sb = sb.tile([P, CHUNKS, P, PACK], F32, name="y_sb", tag="w2_hi")
+        col_bank = ps.tile([P, V // P, P], F32, name="col_bank", tag="b2")
+        for b in range(V // P):
+            nc.tensor.transpose(col_bank[:, b, :], phi_pts[:, b * P : (b + 1) * P], ident[:])
+        phi_col = reuse.tile([P, V // P], F32, name="phi_col", align_bytes=64, offset=12288)
+        nc.scalar.copy(out=phi_col[:], in_=col_bank[:, :, 0])
+
+        y_sb = reuse.tile([P, CHUNKS, P, PACK], F32, name="y_sb", align_bytes=64, offset=15360)
         for c in range(CHUNKS):
             bank = ps.tile([P, PACK, P], F32, name="ya%d" % c, tag="a%d" % c)
-            first_product(bank, w1_codes, w1_scales, xw, xs, X_ROW, c)
+            first_product(bank, w1_codes, w1_scales, xw[:, c * P : (c + 1) * P], xs, X_ROW, c)
             nc.scalar.copy(out=y_sb[:, c], in_=bank[:].rearrange("p j t -> p t j"))
 
         w2_codes, w2_scales = quantize("w2", w2_bf)
-        ew = reuse.tile([P, S], U32, name="ew", align_bytes=64, offset=4096)
-        vw = reuse.tile([P, V], U32, name="vw", align_bytes=64, offset=6144)
+        ew = [reuse.tile([P, S // 2], U32, name="ew%d" % h, align_bytes=64, offset=4096 + 1024 * h) for h in range(2)]
+        vw = reuse.tile([P, V], U32, name="vw", align_bytes=64, offset=7168)
         for h in range(2):
             nc.vector.tensor_copy(
-                ew[:, 256 * h : 256 * (h + 1)], ew_tab[:].bitcast(U32).indirect(coef_sb[:, 16 * h : 16 * (h + 1)])
+                ew[h][:], ew_tab[:].bitcast(U32).indirect(coef_sb[:, 16 * h : 16 * (h + 1)])
             )
         e_banks = []
         for c in range(CHUNKS):
             bank = ps.tile([P, PACK, P], F32, name="yb%d" % c, tag="b%d" % c)
-            first_product(bank, w2_codes, w2_scales, ew, es, E_ROW, c)
+            first_product(bank, w2_codes, w2_scales, ew[c // 2][:, (c % 2) * P : (c % 2 + 1) * P], es, E_ROW, c)
             e_banks.append(bank)
         nc.vector.tensor_copy(vw[:], vw_tab[:].bitcast(U32).indirect(pts_sb[:]))
 
-        z_bf = [sb.tile([P, P, PACK], BF16, name="z_bf%d" % c, align_bytes=64) for c in range(CHUNKS)]
+        z_bf = [
+            reuse.tile([P, P, PACK], BF16, name="z_bf%d" % c, align_bytes=64, offset=4608 + 1024 * c) for c in range(2)
+        ]
+        z_bf.extend([sb.tile([P, P, PACK], BF16, name="z_bf%d" % c, align_bytes=64) for c in range(2, CHUNKS)])
         z_codes = [sb.tile([P, P], U32, name="z_codes%d" % c, align_bytes=64) for c in range(CHUNKS)]
         z_scales = [sb.tile([P, P], U8, name="z_scales%d" % c, align_bytes=64) for c in range(CHUNKS)]
         scaled = [sb.tile([P, V], F32, name="scaled%d" % c) for c in range(CHUNKS)]
@@ -188,22 +198,56 @@ def tile_picked_ymionet_val_p_kernel(
                 stop=True,
             )
 
+        def product_turned(c):
+            bank = ps.tile([P, V // P, P], F32, name="turn%d" % c, tag="a%d" % c)
+            for b in range(V // P):
+                pts_cols = slice(b * P, (b + 1) * P)
+                nc.tensor.matmul_mx(
+                    out=bank[:, b, :],
+                    lhsT=vw[:, pts_cols].bitcast(FP8X4),
+                    lhsT_scale=vs[V_ROW:P, pts_cols],
+                    rhs=z_codes[c][:].bitcast(FP8X4),
+                    rhs_scale=z_scales[c][:],
+                    start=True,
+                    stop=True,
+                )
+            for b in range(V // P):
+                nc.scalar.activation(
+                    scaled[c][:, b * P : (b + 1) * P], bank[:, b, :], COPY, scale=phi_col[:, b : b + 1]
+                )
+
+        def turn_back(c):
+            ss[c] = ps.tile([P, V], F32, name="back%d" % c, tag="b%d" % c)
+            for b in range(V // P):
+                nc.tensor.transpose(ss[c][:, b * P : (b + 1) * P], scaled[c][:, b * P : (b + 1) * P], ident[:])
+
         def scale(c):
             nc.vector.tensor_tensor(scaled[c][:], ss[c][:], phi_pts[:], MULT)
 
-        def finish(engine, c):
-            engine.tensor_tensor(result[c][:], scaled[c][:], lift_sb[c], ADD)
-            nc.sync.dma_start(out=out[c * P : (c + 1) * P, :], in_=result[c][:])
+        def finish(c, src, cols):
+            nc.vector.tensor_tensor(result[c][:, cols], src[:, cols], lift_sb[c][:, cols], ADD)
+            nc.sync.dma_start(out=out[c * P : (c + 1) * P, cols], in_=result[c][:, cols])
 
-        make_z(0)
-        for c in range(CHUNKS):
-            if c + 1 < CHUNKS:
-                make_z(c + 1)
-            quantize_z(c)
-            product_plain(c)
-        scale(0)
-        finish(nc.gpsimd, 0)
-        for c in range(1, CHUNKS):
-            scale(c)
-        for c in range(1, CHUNKS):
-            finish(nc.vector, c)
+        first, second, third, last = 2, 3, 0, 1
+        whole = slice(0, V)
+        make_z(first)
+        make_z(second)
+        quantize_z(first)
+        product_plain(first)
+        make_z(third)
+        quantize_z(second)
+        product_turned(second)
+        make_z(last)
+        quantize_z(third)
+        product_turned(third)
+        scale(first)
+        quantize_z(last)
+        product_turned(last)
+        turn_back(second)
+        turn_back(third)
+        turn_back(last)
+        finish(first, scaled[first], whole)
+        finish(second, ss[second], whole)
+        finish(third, ss[third], whole)
+        for h in range(2):
+            finish(last, ss[last], slice(h * V // 2, (h + 1) * V // 2))

@@ -65,8 +65,8 @@ def tile_picked_ymionet_val_p_kernel(
                 in_=raw[:].rearrange("p j (m t) -> p m j t", t=PACK),
             )
 
-        def quantize(name, grouped):
-            codes = sb.tile([P, H], U32, name=name + "_codes", align_bytes=64)
+        def quantize(name, grouped, offset):
+            codes = reuse.tile([P, H], U32, name=name + "_codes", align_bytes=64, offset=offset)
             scales = sb.tile([P, H], U8, name=name + "_scales", align_bytes=64)
             nc.vector.quantize_mx(out=codes[:].bitcast(FP8X4), scales=scales[:], in_=grouped[:])
             return codes, scales
@@ -121,11 +121,11 @@ def tile_picked_ymionet_val_p_kernel(
         w1_bf = reuse.tile([P, H * PACK], BF16, name="w1_bf", align_bytes=64, offset=0)
         cast_weight(w1_bf, w1_lo, 0, H // 2)
         cast_weight(w1_bf, w1_hi, H // 2, H)
-        w1_codes, w1_scales = quantize("w1", w1_bf)
-        vs = reuse.tile([P, V], U8, name="vs", align_bytes=64, offset=0)
+        vs = reuse.tile([P, V], U8, name="vs", align_bytes=64, offset=28672)
         nc.vector.tensor_copy(vs[:], vs_tab[:].indirect(pts_sb[:]))
         w2_bf = reuse.tile([P, H * PACK], BF16, name="w2_bf", align_bytes=64, offset=4096)
         cast_weight(w2_bf, w2_lo, 0, H // 2)
+        w1_codes, w1_scales = quantize("w1", w1_bf, 36864)
         cast_weight(w2_bf, w2_hi, H // 2, H)
 
         def first_product(bank, codes, scales, words, word_scales, row, c):
@@ -149,12 +149,12 @@ def tile_picked_ymionet_val_p_kernel(
         nc.scalar.copy(out=phi_col[:], in_=col_bank[:, :, 0])
 
         y_sb = reuse.tile([P, CHUNKS, P, PACK], F32, name="y_sb", align_bytes=64, offset=15360)
-        for c in range(CHUNKS):
+        for c in (2, 3, 0, 1):
             bank = ps.tile([P, PACK, P], F32, name="ya%d" % c, tag="a%d" % c)
             first_product(bank, w1_codes, w1_scales, xw[:, c * P : (c + 1) * P], xs, X_ROW, c)
             nc.scalar.copy(out=y_sb[:, c], in_=bank[:].rearrange("p j t -> p t j"))
 
-        w2_codes, w2_scales = quantize("w2", w2_bf)
+        w2_codes, w2_scales = quantize("w2", w2_bf, 40960)
         ew = [reuse.tile([P, S // 2], U32, name="ew%d" % h, align_bytes=64, offset=4096 + 1024 * h) for h in range(2)]
         vw = reuse.tile([P, V], U32, name="vw", align_bytes=64, offset=7168)
         for h in range(2):
@@ -167,6 +167,17 @@ def tile_picked_ymionet_val_p_kernel(
             first_product(bank, w2_codes, w2_scales, ew[c // 2][:, (c % 2) * P : (c % 2 + 1) * P], es, E_ROW, c)
             e_banks.append(bank)
         nc.vector.tensor_copy(vw[:], vw_tab[:].bitcast(U32).indirect(pts_sb[:]))
+        warm = ps.tile([P, V], F32, name="warm", tag="a1")
+        for h in range(2):
+            nc.tensor.matmul_mx(
+                out=warm[:],
+                lhsT=w2_codes[:, h * P : (h + 1) * P].bitcast(FP8X4),
+                lhsT_scale=w2_scales[:, h * P : (h + 1) * P],
+                rhs=vw[:].bitcast(FP8X4),
+                rhs_scale=vs[V_ROW:P, :],
+                start=True,
+                stop=True,
+            )
 
         z_bf = [
             reuse.tile([P, P, PACK], BF16, name="z_bf%d" % c, align_bytes=64, offset=4608 + 1024 * c) for c in range(2)

@@ -19,8 +19,31 @@ COPY = mybir.ActivationFunctionType.Copy
 
 P = 128
 PACK = 4
+QUADRANT = 32
+LIST_ROWS = 16
 CHUNKS = S // P
+POINT_BLOCKS = V // P
+ALIGN = 64
+
 X_ROW, E_ROW, V_ROW = 0, 4, 8
+
+FIRST, SECOND, THIRD, LAST = 2, 3, 0, 1
+
+PHI_COLS_AT = 0
+W1_BF_AT = PHI_COLS_AT
+W2_BF_AT = 4096
+W2_HI_AT = 12288
+VW_AT = W2_HI_AT - 2048 + ALIGN
+EW_AT = W2_HI_AT + ALIGN
+PHI_COL_AT = W2_HI_AT + 3072 - ALIGN
+Y_AT = W2_HI_AT + 3072
+Z_HELD_AT = EW_AT + 512
+W1_LO_AT = 28672
+VS_AT = W1_LO_AT
+W1_HI_AT = 32768
+W2_LO_AT = 36864
+W1_CODES_AT = W2_LO_AT
+W2_CODES_AT = 40960
 
 
 def tile_picked_ymionet_val_p_kernel(
@@ -30,44 +53,44 @@ def tile_picked_ymionet_val_p_kernel(
     with ExitStack() as ctx:
         lists = ctx.enter_context(tc.tile_pool(name="lists", bufs=1))
         sb = ctx.enter_context(tc.tile_pool(name="sb", bufs=1))
-        reuse = ctx.enter_context(tc.tile_pool(name="reuse", bufs=1))
+        placed = ctx.enter_context(tc.tile_pool(name="placed", bufs=1))
         ps = ctx.enter_context(tc.psum_pool(name="ps", bufs=1))
 
         def scale_table(name, width):
-            tile = sb.tile([P, width], U8, name=name, align_bytes=64)
+            tile = sb.tile([P, width], U8, name=name, align_bytes=ALIGN)
             nc.gpsimd.memset(tile[:].bitcast(I32), 0)
             return tile
 
         def load_scales(queues, tile, scales, row):
             for r in range(4):
                 queues[r].dma_start(
-                    out=tile[row + r : P : 32, :].bitcast(I32), in_=scales[0, r:16:4, :].bitcast(I32)
+                    out=tile[row + r : P : QUADRANT, :].bitcast(I32), in_=scales[0, r:16:4, :].bitcast(I32)
                 )
 
         def load_list(name, src):
-            tile = lists.tile([P, S // 16], U16, name=name)
+            tile = lists.tile([P, S // LIST_ROWS], U16, name=name)
             nc.sync.dma_start(tile[:], src)
             return tile
 
         def load_words(name, words, width):
-            tile = sb.tile([P, width], I32, name=name, align_bytes=64)
+            tile = sb.tile([P, width], I32, name=name, align_bytes=ALIGN)
             nc.sync.dma_start(out=tile[:], in_=words[0].rearrange("p n t -> p (n t)").bitcast(I32))
             return tile
 
         def load_weight(name, w, c0, c1, offset):
-            tile = reuse.tile([P, PACK, c1 - c0], F32, name=name, align_bytes=64, offset=offset)
+            tile = placed.tile([P, PACK, c1 - c0], F32, name=name, align_bytes=ALIGN, offset=offset)
             nc.sync.dma_start(out=tile[:], in_=w.rearrange("(p j) c -> p j c", j=PACK)[:, :, c0:c1])
             return tile
 
         def cast_weight(grouped, raw, c0, c1):
             nc.scalar.copy(
-                out=grouped[:].rearrange("p (t m j) -> p m j t", t=PACK, j=PACK)[:, c0 // PACK : c1 // PACK],
-                in_=raw[:].rearrange("p j (m t) -> p m j t", t=PACK),
+                out=grouped[:].rearrange("p (r m j) -> p m j r", r=PACK, j=PACK)[:, c0 // PACK : c1 // PACK],
+                in_=raw[:].rearrange("p j (m r) -> p m j r", r=PACK),
             )
 
-        def quantize(name, grouped, offset):
-            codes = reuse.tile([P, H], U32, name=name + "_codes", align_bytes=64, offset=offset)
-            scales = sb.tile([P, H], U8, name=name + "_scales", align_bytes=64)
+        def quantize_weight(name, grouped, offset):
+            codes = placed.tile([P, H], U32, name=name + "_codes", align_bytes=ALIGN, offset=offset)
+            scales = sb.tile([P, H], U8, name=name + "_scales", align_bytes=ALIGN)
             nc.vector.quantize_mx(out=codes[:].bitcast(FP8X4), scales=scales[:], in_=grouped[:])
             return codes, scales
 
@@ -80,28 +103,29 @@ def tile_picked_ymionet_val_p_kernel(
 
         offs_sb = load_list("offs_sb", offs)
         load_scales([nc.scalar, nc.scalar, nc.sync, nc.sync], xs_tab, x_scales, X_ROW)
-        phi_cols = reuse.tile([P, G // P], F32, name="phi_cols", align_bytes=64, offset=0)
+        phi_cols = placed.tile([P, G // P], F32, name="phi_cols", align_bytes=ALIGN, offset=PHI_COLS_AT)
         nc.scalar.dma_start(out=phi_cols[:], in_=phi[0].rearrange("(p c) -> p c", p=P))
         xw_tab = load_words("xw_tab", x_words, T)
-        w1_lo = load_weight("w1_lo", w1, 0, H // 2, 28672)
+        w1_lo = load_weight("w1_lo", w1, 0, H // 2, W1_LO_AT)
         coef_sb = load_list("coef_sb", coef)
         load_scales([nc.sync] * 4, es_tab, e_scales, E_ROW)
         pts_sb = load_list("pts_sb", pts)
-        w1_hi = load_weight("w1_hi", w1, H // 2, H, 32768)
-        w2_lo = load_weight("w2_lo", w2, 0, H // 2, 36864)
+        w1_hi = load_weight("w1_hi", w1, H // 2, H, W1_HI_AT)
+        w2_lo = load_weight("w2_lo", w2, 0, H // 2, W2_LO_AT)
         load_scales([nc.sync] * 4, vs_tab, v_scales, V_ROW)
-        w2_hi = load_weight("w2_hi", w2, H // 2, H, 12288)
+        w2_hi = load_weight("w2_hi", w2, H // 2, H, W2_HI_AT)
         ew_tab = load_words("ew_tab", e_words, W)
         vw_tab = load_words("vw_tab", v_words, G)
-        lift_sb = []
-        for h in range(2):
+        lift_sb = [None] * CHUNKS
+        for h in (FIRST // 2, THIRD // 2):
             tile = sb.tile([P, 2, V], F32, name="lift%d" % h)
             nc.sync.dma_start(out=tile[:], in_=lift[2 * P * h : 2 * P * (h + 1), :].rearrange("(c p) v -> p c v", p=P))
-            lift_sb.extend([tile[:, c, :] for c in range(2)])
+            for c in range(2):
+                lift_sb[2 * h + c] = tile[:, c, :]
 
-        xs = sb.tile([P, S], U8, name="xs", align_bytes=64)
-        es = sb.tile([P, S], U8, name="es", align_bytes=64)
-        xw = sb.tile([P, S], U32, name="xw", align_bytes=64)
+        xs = sb.tile([P, S], U8, name="xs", align_bytes=ALIGN)
+        es = sb.tile([P, S], U8, name="es", align_bytes=ALIGN)
+        xw = sb.tile([P, S], U32, name="xw", align_bytes=ALIGN)
         phi_pts = sb.tile([P, V], F32, name="phi_pts")
 
         phi_tab = sb.tile([P, G], F32, name="phi_tab")
@@ -118,147 +142,149 @@ def tile_picked_ymionet_val_p_kernel(
         nc.vector.tensor_copy(xw[:], xw_tab[:].bitcast(U32).indirect(offs_sb[:]))
         nc.vector.tensor_copy(es[:], es_tab[:].indirect(coef_sb[:]))
         nc.vector.tensor_copy(phi_pts[:], phi_tab[:].indirect(pts_sb[:]))
-        w1_bf = reuse.tile([P, H * PACK], BF16, name="w1_bf", align_bytes=64, offset=0)
+        w1_bf = placed.tile([P, H * PACK], BF16, name="w1_bf", align_bytes=ALIGN, offset=W1_BF_AT)
         cast_weight(w1_bf, w1_lo, 0, H // 2)
         cast_weight(w1_bf, w1_hi, H // 2, H)
-        vs = reuse.tile([P, V], U8, name="vs", align_bytes=64, offset=28672)
+        vs = placed.tile([P, V], U8, name="vs", align_bytes=ALIGN, offset=VS_AT)
         nc.vector.tensor_copy(vs[:], vs_tab[:].indirect(pts_sb[:]))
-        w2_bf = reuse.tile([P, H * PACK], BF16, name="w2_bf", align_bytes=64, offset=4096)
+        w2_bf = placed.tile([P, H * PACK], BF16, name="w2_bf", align_bytes=ALIGN, offset=W2_BF_AT)
         cast_weight(w2_bf, w2_lo, 0, H // 2)
-        w1_codes, w1_scales = quantize("w1", w1_bf, 36864)
+        w1_codes, w1_scales = quantize_weight("w1", w1_bf, W1_CODES_AT)
         cast_weight(w2_bf, w2_hi, H // 2, H)
 
-        def first_product(bank, codes, scales, words, word_scales, row, c):
-            cols = slice(c * P, (c + 1) * P)
-            for j in range(PACK):
-                hid = slice(j * P, (j + 1) * P)
+        def first_product(bank, codes, scales, words, word_scales):
+            for r in range(PACK):
+                hid = slice(r * P, (r + 1) * P)
                 nc.tensor.matmul_mx(
-                    out=bank[:, j, :],
+                    out=bank[:, r, :],
                     lhsT=codes[:, hid].bitcast(FP8X4),
                     lhsT_scale=scales[:, hid],
                     rhs=words.bitcast(FP8X4),
-                    rhs_scale=word_scales[row:P, cols],
+                    rhs_scale=word_scales,
                     start=True,
                     stop=True,
                 )
 
-        col_bank = ps.tile([P, V // P, P], F32, name="col_bank", tag="b2")
-        for b in range(V // P):
+        col_bank = ps.tile([P, POINT_BLOCKS, P], F32, name="col_bank", tag="b2")
+        for b in range(POINT_BLOCKS):
             nc.tensor.transpose(col_bank[:, b, :], phi_pts[:, b * P : (b + 1) * P], ident[:])
-        phi_col = reuse.tile([P, V // P], F32, name="phi_col", align_bytes=64, offset=12288)
+        phi_col = placed.tile([P, POINT_BLOCKS], F32, name="phi_col", align_bytes=ALIGN, offset=PHI_COL_AT)
         nc.scalar.copy(out=phi_col[:], in_=col_bank[:, :, 0])
 
-        y_sb = reuse.tile([P, CHUNKS, P, PACK], F32, name="y_sb", align_bytes=64, offset=15360)
-        for c in (2, 3, 0, 1):
-            bank = ps.tile([P, PACK, P], F32, name="ya%d" % c, tag="a%d" % c)
-            first_product(bank, w1_codes, w1_scales, xw[:, c * P : (c + 1) * P], xs, X_ROW, c)
-            nc.scalar.copy(out=y_sb[:, c], in_=bank[:].rearrange("p j t -> p t j"))
+        y_sb = placed.tile([P, CHUNKS, P, PACK], F32, name="y_sb", align_bytes=ALIGN, offset=Y_AT)
+        for c in (FIRST, SECOND, THIRD, LAST):
+            entries = slice(c * P, (c + 1) * P)
+            bank = ps.tile([P, PACK, P], F32, name="y_bank%d" % c, tag="a%d" % c)
+            first_product(bank, w1_codes, w1_scales, xw[:, entries], xs[X_ROW:P, entries])
+            nc.scalar.copy(out=y_sb[:, c], in_=bank[:].rearrange("p r t -> p t r"))
 
-        w2_codes, w2_scales = quantize("w2", w2_bf, 40960)
-        ew = [reuse.tile([P, S // 2], U32, name="ew%d" % h, align_bytes=64, offset=4096 + 1024 * h) for h in range(2)]
-        vw = reuse.tile([P, V], U32, name="vw", align_bytes=64, offset=7168)
+        w2_codes, w2_scales = quantize_weight("w2", w2_bf, W2_CODES_AT)
+        half = S // 2
+        ew = [
+            placed.tile([P, half], U32, name="ew%d" % h, align_bytes=ALIGN, offset=EW_AT + 4 * half * h)
+            for h in range(2)
+        ]
+        vw = placed.tile([P, V], U32, name="vw", align_bytes=ALIGN, offset=VW_AT)
         for h in range(2):
-            nc.vector.tensor_copy(
-                ew[h][:], ew_tab[:].bitcast(U32).indirect(coef_sb[:, 16 * h : 16 * (h + 1)])
-            )
+            offsets = coef_sb[:, h * half // LIST_ROWS : (h + 1) * half // LIST_ROWS]
+            nc.vector.tensor_copy(ew[h][:], ew_tab[:].bitcast(U32).indirect(offsets))
         e_banks = []
         for c in range(CHUNKS):
-            bank = ps.tile([P, PACK, P], F32, name="yb%d" % c, tag="b%d" % c)
-            first_product(bank, w2_codes, w2_scales, ew[c // 2][:, (c % 2) * P : (c % 2 + 1) * P], es, E_ROW, c)
+            bank = ps.tile([P, PACK, P], F32, name="e_bank%d" % c, tag="b%d" % c)
+            words = ew[c // 2][:, (c % 2) * P : (c % 2 + 1) * P]
+            first_product(bank, w2_codes, w2_scales, words, es[E_ROW:P, c * P : (c + 1) * P])
             e_banks.append(bank)
         nc.vector.tensor_copy(vw[:], vw_tab[:].bitcast(U32).indirect(pts_sb[:]))
-        warm = ps.tile([P, V], F32, name="warm", tag="a1")
-        for h in range(2):
+
+        warm = ps.tile([P, V], F32, name="warm", tag="a%d" % LAST)
+        for r in range(2):
             nc.tensor.matmul_mx(
                 out=warm[:],
-                lhsT=w2_codes[:, h * P : (h + 1) * P].bitcast(FP8X4),
-                lhsT_scale=w2_scales[:, h * P : (h + 1) * P],
+                lhsT=w2_codes[:, r * P : (r + 1) * P].bitcast(FP8X4),
+                lhsT_scale=w2_scales[:, r * P : (r + 1) * P],
                 rhs=vw[:].bitcast(FP8X4),
                 rhs_scale=vs[V_ROW:P, :],
                 start=True,
                 stop=True,
             )
 
+        z_bytes = P * PACK * 2
         z_bf = [
-            reuse.tile([P, P, PACK], BF16, name="z_bf%d" % c, align_bytes=64, offset=4608 + 1024 * c) for c in range(2)
+            placed.tile([P, P, PACK], BF16, name="z_bf%d" % c, align_bytes=ALIGN, offset=Z_HELD_AT + z_bytes * c)
+            for c in range(2)
         ]
-        z_bf.extend([sb.tile([P, P, PACK], BF16, name="z_bf%d" % c, align_bytes=64) for c in range(2, CHUNKS)])
-        z_codes = [sb.tile([P, P], U32, name="z_codes%d" % c, align_bytes=64) for c in range(CHUNKS)]
-        z_scales = [sb.tile([P, P], U8, name="z_scales%d" % c, align_bytes=64) for c in range(CHUNKS)]
-        scaled = [sb.tile([P, V], F32, name="scaled%d" % c) for c in range(CHUNKS)]
+        z_bf.extend([sb.tile([P, P, PACK], BF16, name="z_bf%d" % c, align_bytes=ALIGN) for c in range(2, CHUNKS)])
+        z_codes = [sb.tile([P, P], U32, name="z_codes%d" % c, align_bytes=ALIGN) for c in range(CHUNKS)]
+        z_scales = [sb.tile([P, P], U8, name="z_scales%d" % c, align_bytes=ALIGN) for c in range(CHUNKS)]
+        turned = [sb.tile([P, POINT_BLOCKS, P], F32, name="turned%d" % c) for c in range(CHUNKS)]
         result = [sb.tile([P, V], F32, name="result%d" % c) for c in range(CHUNKS)]
-        ss = [None] * CHUNKS
 
         def make_z(c):
-            nc.vector.tensor_tensor(z_bf[c][:], e_banks[c][:].rearrange("p j t -> p t j"), y_sb[:, c], MULT)
+            nc.vector.tensor_tensor(z_bf[c][:], e_banks[c][:].rearrange("p r t -> p t r"), y_sb[:, c], MULT)
 
         def quantize_z(c):
             nc.vector.quantize_mx(
-                out=z_codes[c][:].bitcast(FP8X4), scales=z_scales[c][:], in_=z_bf[c][:].rearrange("p t j -> p (t j)")
+                out=z_codes[c][:].bitcast(FP8X4), scales=z_scales[c][:], in_=z_bf[c][:].rearrange("p t r -> p (t r)")
             )
 
-        def product_plain(c):
-            ss[c] = ps.tile([P, V], F32, name="ss%d" % c, tag="a%d" % c)
-            nc.tensor.matmul_mx(
-                out=ss[c][:],
-                lhsT=z_codes[c][:].bitcast(FP8X4),
-                lhsT_scale=z_scales[c][:],
-                rhs=vw[:].bitcast(FP8X4),
-                rhs_scale=vs[V_ROW:P, :],
-                start=True,
-                stop=True,
-            )
-
-        def product_turned(c):
-            bank = ps.tile([P, V // P, P], F32, name="turn%d" % c, tag="a%d" % c)
-            for b in range(V // P):
-                pts_cols = slice(b * P, (b + 1) * P)
+        def product_turned(c, blocks):
+            bank = ps.tile([P, POINT_BLOCKS, P], F32, name="turned_bank%d" % c, tag="a%d" % c)
+            for b in blocks:
+                points = slice(b * P, (b + 1) * P)
                 nc.tensor.matmul_mx(
                     out=bank[:, b, :],
-                    lhsT=vw[:, pts_cols].bitcast(FP8X4),
-                    lhsT_scale=vs[V_ROW:P, pts_cols],
+                    lhsT=vw[:, points].bitcast(FP8X4),
+                    lhsT_scale=vs[V_ROW:P, points],
                     rhs=z_codes[c][:].bitcast(FP8X4),
                     rhs_scale=z_scales[c][:],
                     start=True,
                     stop=True,
                 )
-            for b in range(V // P):
-                nc.scalar.activation(
-                    scaled[c][:, b * P : (b + 1) * P], bank[:, b, :], COPY, scale=phi_col[:, b : b + 1]
-                )
+            for b in blocks:
+                nc.scalar.activation(turned[c][:, b, :], bank[:, b, :], COPY, scale=phi_col[:, b : b + 1])
 
-        def turn_back(c):
-            ss[c] = ps.tile([P, V], F32, name="back%d" % c, tag="b%d" % c)
-            for b in range(V // P):
-                nc.tensor.transpose(ss[c][:, b * P : (b + 1) * P], scaled[c][:, b * P : (b + 1) * P], ident[:])
+        def turn_back(c, blocks):
+            bank = ps.tile([P, V], F32, name="back_bank%d" % c, tag="b%d" % c)
+            for b in blocks:
+                nc.tensor.transpose(bank[:, b * P : (b + 1) * P], turned[c][:, b, :], ident[:])
+            return bank
 
-        def scale(c):
-            nc.vector.tensor_tensor(scaled[c][:], ss[c][:], phi_pts[:], MULT)
+        def finish(c, scaled, points):
+            nc.vector.tensor_tensor(result[c][:, points], scaled, lift_sb[c][:, points], ADD)
+            nc.sync.dma_start(out=out[c * P : (c + 1) * P, points], in_=result[c][:, points])
 
-        def finish(c, src, cols):
-            nc.vector.tensor_tensor(result[c][:, cols], src[:, cols], lift_sb[c][:, cols], ADD)
-            nc.sync.dma_start(out=out[c * P : (c + 1) * P, cols], in_=result[c][:, cols])
-
-        first, second, third, last = 2, 3, 0, 1
-        whole = slice(0, V)
-        make_z(first)
-        make_z(second)
-        quantize_z(first)
-        product_plain(first)
-        make_z(third)
-        quantize_z(second)
-        product_turned(second)
-        make_z(last)
-        quantize_z(third)
-        product_turned(third)
-        scale(first)
-        quantize_z(last)
-        product_turned(last)
-        turn_back(second)
-        turn_back(third)
-        turn_back(last)
-        finish(first, scaled[first], whole)
-        finish(second, ss[second], whole)
-        finish(third, ss[third], whole)
-        for h in range(2):
-            finish(last, ss[last], slice(h * V // 2, (h + 1) * V // 2))
+        whole, left, right = slice(0, V), slice(0, V // 2), slice(V // 2, V)
+        all_blocks, right_blocks = range(POINT_BLOCKS), range(POINT_BLOCKS // 2, POINT_BLOCKS)
+        make_z(FIRST)
+        make_z(SECOND)
+        quantize_z(FIRST)
+        product_turned(FIRST, all_blocks)
+        make_z(THIRD)
+        quantize_z(SECOND)
+        product_turned(SECOND, all_blocks)
+        back_first = turn_back(FIRST, all_blocks)
+        make_z(LAST)
+        quantize_z(THIRD)
+        product_turned(THIRD, all_blocks)
+        quantize_z(LAST)
+        plain_bank = ps.tile([P, V // 2], F32, name="plain_bank", tag="a%d" % FIRST)
+        nc.tensor.matmul_mx(
+            out=plain_bank[:],
+            lhsT=z_codes[LAST][:].bitcast(FP8X4),
+            lhsT_scale=z_scales[LAST][:],
+            rhs=vw[:, left].bitcast(FP8X4),
+            rhs_scale=vs[V_ROW:P, left],
+            start=True,
+            stop=True,
+        )
+        product_turned(LAST, right_blocks)
+        back_second = turn_back(SECOND, all_blocks)
+        back_third = turn_back(THIRD, all_blocks)
+        back_last = turn_back(LAST, right_blocks)
+        finish(FIRST, back_first[:], whole)
+        plain_scaled = sb.tile([P, V // 2], F32, name="plain_scaled")
+        nc.vector.tensor_tensor(plain_scaled[:], plain_bank[:], phi_pts[:, left], MULT)
+        finish(SECOND, back_second[:], whole)
+        finish(LAST, plain_scaled[:], left)
+        finish(THIRD, back_third[:], whole)
+        finish(LAST, back_last[:, right], right)

@@ -196,18 +196,6 @@ def tile_picked_ymionet_val_p_kernel(
             e_banks.append(bank)
         nc.vector.tensor_copy(vw[:], vw_tab[:].bitcast(U32).indirect(pts_sb[:]))
 
-        warm = ps.tile([P, V], F32, name="warm", tag="a%d" % LAST)
-        for r in range(2):
-            nc.tensor.matmul_mx(
-                out=warm[:],
-                lhsT=w2_codes[:, r * P : (r + 1) * P].bitcast(FP8X4),
-                lhsT_scale=w2_scales[:, r * P : (r + 1) * P],
-                rhs=vw[:].bitcast(FP8X4),
-                rhs_scale=vs[V_ROW:P, :],
-                start=True,
-                stop=True,
-            )
-
         z_bytes = P * PACK * 2
         z_bf = [
             placed.tile([P, P, PACK], BF16, name="z_bf%d" % c, align_bytes=ALIGN, offset=Z_HELD_AT + z_bytes * c)

@@ -27,23 +27,16 @@ ALIGN = 64
 
 X_ROW, E_ROW, V_ROW = 0, 4, 8
 
-FIRST, SECOND, THIRD, LAST = 2, 3, 0, 1
+FIRST, SECOND, THIRD, LAST = 0, 1, 2, 3
 
-PHI_COLS_AT = 0
-W1_BF_AT = PHI_COLS_AT
-W2_BF_AT = 4096
-W2_HI_AT = 12288
-VW_AT = W2_HI_AT - 2048 + ALIGN
-EW_AT = W2_HI_AT + ALIGN
-PHI_COL_AT = W2_HI_AT + 3072 - ALIGN
-Y_AT = W2_HI_AT + 3072
-Z_HELD_AT = EW_AT + 512
-W1_LO_AT = 28672
-VS_AT = W1_LO_AT
-W1_HI_AT = 32768
-W2_LO_AT = 36864
-W1_CODES_AT = W2_LO_AT
-W2_CODES_AT = 40960
+W2_AT = 0
+PHI_COL_AT = W2_AT
+Y_AT = W2_AT + ALIGN
+VS_TAB_AT = 16384
+W1_CODES_AT = VS_TAB_AT
+VW_TAB_AT = 20480
+W2_CODES_AT = VW_TAB_AT
+E_PIECES = ((0, 128), (128, 256), (256, 512))
 
 
 def tile_picked_ymionet_val_p_kernel(
@@ -56,10 +49,8 @@ def tile_picked_ymionet_val_p_kernel(
         placed = ctx.enter_context(tc.tile_pool(name="placed", bufs=1))
         ps = ctx.enter_context(tc.psum_pool(name="ps", bufs=1))
 
-        def scale_table(name, width):
-            tile = sb.tile([P, width], U8, name=name, align_bytes=ALIGN)
-            nc.gpsimd.memset(tile[:].bitcast(I32), 0)
-            return tile
+        def scale_table(tile, engine):
+            engine.memset(tile[:].bitcast(I32), 0)
 
         def load_scales(queues, tile, scales, row):
             for r in range(4):
@@ -72,50 +63,50 @@ def tile_picked_ymionet_val_p_kernel(
             nc.sync.dma_start(tile[:], src)
             return tile
 
-        def load_words(name, words, width):
-            tile = sb.tile([P, width], I32, name=name, align_bytes=ALIGN)
+        def load_words(tile, words):
             nc.sync.dma_start(out=tile[:], in_=words[0].rearrange("p n t -> p (n t)").bitcast(I32))
-            return tile
 
-        def load_weight(name, w, c0, c1, offset):
-            tile = placed.tile([P, PACK, c1 - c0], F32, name=name, align_bytes=ALIGN, offset=offset)
-            nc.sync.dma_start(out=tile[:], in_=w.rearrange("(p j) c -> p j c", j=PACK)[:, :, c0:c1])
-            return tile
+        def load_weight(tile, w):
+            nc.sync.dma_start(out=tile[:], in_=w.rearrange("(p j) c -> p j c", j=PACK))
 
-        def cast_weight(grouped, raw, c0, c1):
-            nc.scalar.copy(
-                out=grouped[:].rearrange("p (r m j) -> p m j r", r=PACK, j=PACK)[:, c0 // PACK : c1 // PACK],
-                in_=raw[:].rearrange("p j (m r) -> p m j r", r=PACK),
+        def cast_weight(copy, grouped, raw, h):
+            copy(
+                out=grouped[:].rearrange("p (r m j) -> p m j r", r=PACK, j=PACK)[:, :, :, 2 * h : 2 * h + 2],
+                in_=raw[:].rearrange("p j (m r) -> p m j r", r=PACK)[:, :, :, 2 * h : 2 * h + 2],
             )
 
-        def quantize_weight(name, grouped, offset):
-            codes = placed.tile([P, H], U32, name=name + "_codes", align_bytes=ALIGN, offset=offset)
-            scales = sb.tile([P, H], U8, name=name + "_scales", align_bytes=ALIGN)
-            nc.vector.quantize_mx(out=codes[:].bitcast(FP8X4), scales=scales[:], in_=grouped[:])
-            return codes, scales
+        def quantize_weight(codes, scales, grouped):
+            nc.vector.quantize_mx(out=codes.bitcast(FP8X4), scales=scales, in_=grouped)
 
-        xs_tab = scale_table("xs_tab", T)
-        es_tab = scale_table("es_tab", W)
-        vs_tab = scale_table("vs_tab", G)
+        xs_tab = sb.tile([P, T], U8, name="xs_tab", align_bytes=ALIGN)
+        vs_tab = placed.tile([P, G], U8, name="vs_tab", align_bytes=ALIGN, offset=VS_TAB_AT)
+        es_tab = sb.tile([P, W], U8, name="es_tab", align_bytes=ALIGN)
+        xw_tab = sb.tile([P, T], I32, name="xw_tab", align_bytes=ALIGN)
+        vw_tab = placed.tile([P, G], I32, name="vw_tab", align_bytes=ALIGN, offset=VW_TAB_AT)
+        ew_tab = sb.tile([P, W], I32, name="ew_tab", align_bytes=ALIGN)
+        phi_tab = sb.tile([P, G], F32, name="phi_tab")
+        scale_table(xs_tab, nc.gpsimd)
+        scale_table(vs_tab, nc.vector)
+        nc.vector.memset(phi_tab[:], 0.0)
+        scale_table(es_tab, nc.gpsimd)
 
         ident = sb.tile([P, P], F32, name="ident")
         make_identity(nc, ident[:])
 
         offs_sb = load_list("offs_sb", offs)
+        load_words(xw_tab, x_words)
         load_scales([nc.scalar, nc.scalar, nc.sync, nc.sync], xs_tab, x_scales, X_ROW)
-        phi_cols = placed.tile([P, G // P], F32, name="phi_cols", align_bytes=ALIGN, offset=PHI_COLS_AT)
-        nc.scalar.dma_start(out=phi_cols[:], in_=phi[0].rearrange("(p c) -> p c", p=P))
-        xw_tab = load_words("xw_tab", x_words, T)
-        w1_lo = load_weight("w1_lo", w1, 0, H // 2, W1_LO_AT)
+        pts_sb = load_list("pts_sb", pts)
+        w1_raw = sb.tile([P, PACK, H], F32, name="w1_raw", align_bytes=ALIGN)
+        load_weight(w1_raw, w1)
+        load_scales([nc.sync] * 4, vs_tab, v_scales, V_ROW)
+        nc.sync.dma_start(out=phi_tab[0:1, :], in_=phi[0:1, :])
+        w2_raw = placed.tile([P, PACK, H], F32, name="w2_raw", align_bytes=ALIGN, offset=W2_AT)
+        load_weight(w2_raw, w2)
         coef_sb = load_list("coef_sb", coef)
         load_scales([nc.sync] * 4, es_tab, e_scales, E_ROW)
-        pts_sb = load_list("pts_sb", pts)
-        w1_hi = load_weight("w1_hi", w1, H // 2, H, W1_HI_AT)
-        w2_lo = load_weight("w2_lo", w2, 0, H // 2, W2_LO_AT)
-        load_scales([nc.sync] * 4, vs_tab, v_scales, V_ROW)
-        w2_hi = load_weight("w2_hi", w2, H // 2, H, W2_HI_AT)
-        ew_tab = load_words("ew_tab", e_words, W)
-        vw_tab = load_words("vw_tab", v_words, G)
+        load_words(vw_tab, v_words)
+        load_words(ew_tab, e_words)
         lift_sb = [None] * CHUNKS
         for h in (FIRST // 2, THIRD // 2):
             tile = sb.tile([P, 2, V], F32, name="lift%d" % h)
@@ -125,39 +116,40 @@ def tile_picked_ymionet_val_p_kernel(
 
         xs = sb.tile([P, S], U8, name="xs", align_bytes=ALIGN)
         es = sb.tile([P, S], U8, name="es", align_bytes=ALIGN)
+        vs = sb.tile([P, V], U8, name="vs", align_bytes=ALIGN)
         xw = sb.tile([P, S], U32, name="xw", align_bytes=ALIGN)
         phi_pts = sb.tile([P, V], F32, name="phi_pts")
+        w1_bf = sb.tile([P, H * PACK], BF16, name="w1_bf", align_bytes=ALIGN)
+        w2_bf = sb.tile([P, H * PACK], BF16, name="w2_bf", align_bytes=ALIGN)
+        w1_codes = placed.tile([P, H], U32, name="w1_codes", align_bytes=ALIGN, offset=W1_CODES_AT)
+        w2_codes = placed.tile([P, H], U32, name="w2_codes", align_bytes=ALIGN, offset=W2_CODES_AT)
+        vw = sb.tile([P, V], U32, name="vw", align_bytes=ALIGN)
+        ew = sb.tile([P, S], U32, name="ew", align_bytes=ALIGN)
+        w1_scales = sb.tile([P, H], U8, name="w1_scales", align_bytes=ALIGN)
+        w2_scales = sb.tile([P, H], U8, name="w2_scales", align_bytes=ALIGN)
 
-        phi_tab = sb.tile([P, G], F32, name="phi_tab")
-        for h in range(2):
-            bank = ps.tile([P, 4, P], F32, name="phi_bank%d" % h, tag="b%d" % h)
-            for c in range(4):
-                nc.tensor.transpose(bank[:, c, :], phi_cols[:, 4 * h + c : 4 * h + c + 1].to_broadcast([P, P]), ident[:])
-            nc.scalar.copy(
-                out=phi_tab[:].rearrange("m (p c) -> m p c", p=P)[:, :, 4 * h : 4 * h + 4],
-                in_=bank[:].rearrange("m c p -> m p c"),
-            )
-
-        nc.vector.tensor_copy(xs[:], xs_tab[:].indirect(offs_sb[:]))
         nc.vector.tensor_copy(xw[:], xw_tab[:].bitcast(U32).indirect(offs_sb[:]))
-        nc.vector.tensor_copy(es[:], es_tab[:].indirect(coef_sb[:]))
-        nc.vector.tensor_copy(phi_pts[:], phi_tab[:].indirect(pts_sb[:]))
-        w1_bf = placed.tile([P, H * PACK], BF16, name="w1_bf", align_bytes=ALIGN, offset=W1_BF_AT)
-        cast_weight(w1_bf, w1_lo, 0, H // 2)
-        cast_weight(w1_bf, w1_hi, H // 2, H)
-        vs = placed.tile([P, V], U8, name="vs", align_bytes=ALIGN, offset=VS_AT)
+        nc.vector.tensor_copy(xs[:], xs_tab[:].indirect(offs_sb[:]))
+        cast_weight(nc.scalar.copy, w1_bf, w1_raw, 0)
+        cast_weight(nc.vector.tensor_copy, w1_bf, w1_raw, 1)
         nc.vector.tensor_copy(vs[:], vs_tab[:].indirect(pts_sb[:]))
-        w2_bf = placed.tile([P, H * PACK], BF16, name="w2_bf", align_bytes=ALIGN, offset=W2_BF_AT)
-        cast_weight(w2_bf, w2_lo, 0, H // 2)
-        w1_codes, w1_scales = quantize_weight("w1", w1_bf, W1_CODES_AT)
-        cast_weight(w2_bf, w2_hi, H // 2, H)
+        nc.scalar.activation(phi_pts[:], phi_tab[:].indirect(pts_sb[:]), COPY)
+        quantize_weight(w1_codes[:], w1_scales[:], w1_bf[:])
+        nc.vector.tensor_copy(es[:], es_tab[:].indirect(coef_sb[:]))
+        cast_weight(nc.scalar.copy, w2_bf, w2_raw, 0)
+        cast_weight(nc.scalar.copy, w2_bf, w2_raw, 1)
+        nc.vector.tensor_copy(vw[:], vw_tab[:].bitcast(U32).indirect(pts_sb[:]))
+        quantize_weight(w2_codes[:], w2_scales[:], w2_bf[:])
+
+        w1_tiles = [w1_codes[:, r * P : (r + 1) * P] for r in range(PACK)]
+        w2_tiles = [w2_codes[:, r * P : (r + 1) * P] for r in range(PACK)]
 
         def first_product(bank, codes, scales, words, word_scales):
             for r in range(PACK):
                 hid = slice(r * P, (r + 1) * P)
                 nc.tensor.matmul_mx(
                     out=bank[:, r, :],
-                    lhsT=codes[:, hid].bitcast(FP8X4),
+                    lhsT=codes[r].bitcast(FP8X4),
                     lhsT_scale=scales[:, hid],
                     rhs=words.bitcast(FP8X4),
                     rhs_scale=word_scales,
@@ -165,7 +157,7 @@ def tile_picked_ymionet_val_p_kernel(
                     stop=True,
                 )
 
-        col_bank = ps.tile([P, POINT_BLOCKS, P], F32, name="col_bank", tag="b2")
+        col_bank = ps.tile([P, POINT_BLOCKS, P], F32, name="col_bank", tag="a%d" % LAST)
         for b in range(POINT_BLOCKS):
             nc.tensor.transpose(col_bank[:, b, :], phi_pts[:, b * P : (b + 1) * P], ident[:])
         phi_col = placed.tile([P, POINT_BLOCKS], F32, name="phi_col", align_bytes=ALIGN, offset=PHI_COL_AT)
@@ -175,33 +167,20 @@ def tile_picked_ymionet_val_p_kernel(
         for c in (FIRST, SECOND, THIRD, LAST):
             entries = slice(c * P, (c + 1) * P)
             bank = ps.tile([P, PACK, P], F32, name="y_bank%d" % c, tag="a%d" % c)
-            first_product(bank, w1_codes, w1_scales, xw[:, entries], xs[X_ROW:P, entries])
+            first_product(bank, w1_tiles, w1_scales, xw[:, entries], xs[X_ROW:P, entries])
             nc.scalar.copy(out=y_sb[:, c], in_=bank[:].rearrange("p r t -> p t r"))
 
-        w2_codes, w2_scales = quantize_weight("w2", w2_bf, W2_CODES_AT)
-        half = S // 2
-        ew = [
-            placed.tile([P, half], U32, name="ew%d" % h, align_bytes=ALIGN, offset=EW_AT + 4 * half * h)
-            for h in range(2)
-        ]
-        vw = placed.tile([P, V], U32, name="vw", align_bytes=ALIGN, offset=VW_AT)
-        for h in range(2):
-            offsets = coef_sb[:, h * half // LIST_ROWS : (h + 1) * half // LIST_ROWS]
-            nc.vector.tensor_copy(ew[h][:], ew_tab[:].bitcast(U32).indirect(offsets))
+        for start, stop in E_PIECES:
+            offsets = coef_sb[:, start // LIST_ROWS : stop // LIST_ROWS]
+            nc.vector.tensor_copy(ew[:, start:stop], ew_tab[:].bitcast(U32).indirect(offsets))
         e_banks = []
         for c in range(CHUNKS):
+            entries = slice(c * P, (c + 1) * P)
             bank = ps.tile([P, PACK, P], F32, name="e_bank%d" % c, tag="b%d" % c)
-            words = ew[c // 2][:, (c % 2) * P : (c % 2 + 1) * P]
-            first_product(bank, w2_codes, w2_scales, words, es[E_ROW:P, c * P : (c + 1) * P])
+            first_product(bank, w2_tiles, w2_scales, ew[:, entries], es[E_ROW:P, entries])
             e_banks.append(bank)
-        nc.vector.tensor_copy(vw[:], vw_tab[:].bitcast(U32).indirect(pts_sb[:]))
 
-        z_bytes = P * PACK * 2
-        z_bf = [
-            placed.tile([P, P, PACK], BF16, name="z_bf%d" % c, align_bytes=ALIGN, offset=Z_HELD_AT + z_bytes * c)
-            for c in range(2)
-        ]
-        z_bf.extend([sb.tile([P, P, PACK], BF16, name="z_bf%d" % c, align_bytes=ALIGN) for c in range(2, CHUNKS)])
+        z_bf = [sb.tile([P, P, PACK], BF16, name="z_bf%d" % c, align_bytes=ALIGN) for c in range(CHUNKS)]
         z_codes = [sb.tile([P, P], U32, name="z_codes%d" % c, align_bytes=ALIGN) for c in range(CHUNKS)]
         z_scales = [sb.tile([P, P], U8, name="z_scales%d" % c, align_bytes=ALIGN) for c in range(CHUNKS)]
         turned = [sb.tile([P, POINT_BLOCKS, P], F32, name="turned%d" % c) for c in range(CHUNKS)]
@@ -231,8 +210,8 @@ def tile_picked_ymionet_val_p_kernel(
             for b in blocks:
                 nc.scalar.activation(turned[c][:, b, :], bank[:, b, :], COPY, scale=phi_col[:, b : b + 1])
 
-        def turn_back(c, blocks):
-            bank = ps.tile([P, V], F32, name="back_bank%d" % c, tag="b%d" % c)
+        def turn_back(c, blocks, tag):
+            bank = ps.tile([P, V], F32, name="back_bank%d_%d" % (c, blocks.start), tag=tag)
             for b in blocks:
                 nc.tensor.transpose(bank[:, b * P : (b + 1) * P], turned[c][:, b, :], ident[:])
             return bank
@@ -242,7 +221,8 @@ def tile_picked_ymionet_val_p_kernel(
             nc.sync.dma_start(out=out[c * P : (c + 1) * P, points], in_=result[c][:, points])
 
         whole, left, right = slice(0, V), slice(0, V // 2), slice(V // 2, V)
-        all_blocks, right_blocks = range(POINT_BLOCKS), range(POINT_BLOCKS // 2, POINT_BLOCKS)
+        all_blocks = range(POINT_BLOCKS)
+        left_blocks, right_blocks = range(POINT_BLOCKS // 2), range(POINT_BLOCKS // 2, POINT_BLOCKS)
         make_z(FIRST)
         make_z(SECOND)
         quantize_z(FIRST)
@@ -250,29 +230,18 @@ def tile_picked_ymionet_val_p_kernel(
         make_z(THIRD)
         quantize_z(SECOND)
         product_turned(SECOND, all_blocks)
-        back_first = turn_back(FIRST, all_blocks)
+        back_first = turn_back(FIRST, all_blocks, "b%d" % FIRST)
         make_z(LAST)
         quantize_z(THIRD)
         product_turned(THIRD, all_blocks)
         quantize_z(LAST)
-        plain_bank = ps.tile([P, V // 2], F32, name="plain_bank", tag="a%d" % FIRST)
-        nc.tensor.matmul_mx(
-            out=plain_bank[:],
-            lhsT=z_codes[LAST][:].bitcast(FP8X4),
-            lhsT_scale=z_scales[LAST][:],
-            rhs=vw[:, left].bitcast(FP8X4),
-            rhs_scale=vs[V_ROW:P, left],
-            start=True,
-            stop=True,
-        )
-        product_turned(LAST, right_blocks)
-        back_second = turn_back(SECOND, all_blocks)
-        back_third = turn_back(THIRD, all_blocks)
-        back_last = turn_back(LAST, right_blocks)
+        product_turned(LAST, all_blocks)
+        back_second = turn_back(SECOND, all_blocks, "b%d" % SECOND)
+        back_third = turn_back(THIRD, all_blocks, "b%d" % THIRD)
+        back_left = turn_back(LAST, left_blocks, "b%d" % LAST)
+        back_right = turn_back(LAST, right_blocks, "a%d" % FIRST)
         finish(FIRST, back_first[:], whole)
-        plain_scaled = sb.tile([P, V // 2], F32, name="plain_scaled")
-        nc.vector.tensor_tensor(plain_scaled[:], plain_bank[:], phi_pts[:, left], MULT)
         finish(SECOND, back_second[:], whole)
-        finish(LAST, plain_scaled[:], left)
         finish(THIRD, back_third[:], whole)
-        finish(LAST, back_last[:, right], right)
+        finish(LAST, back_left[:, left], left)
+        finish(LAST, back_right[:, right], right)

@@ -23,6 +23,7 @@ QUADRANT = 32
 LIST_ROWS = 16
 CHUNKS = S // P
 POINT_BLOCKS = V // P
+SPREAD = 8
 ALIGN = 64
 
 X_ROW, E_ROW, V_ROW = 0, 4, 8
@@ -30,10 +31,12 @@ X_ROW, E_ROW, V_ROW = 0, 4, 8
 FIRST, SECOND, THIRD, LAST = 0, 1, 2, 3
 
 W2_AT = 0
-PHI_COL_AT = W2_AT
-Y_AT = W2_AT + ALIGN
-VS_TAB_AT = 16384
-W1_CODES_AT = VS_TAB_AT
+PHI_LEFT_AT = W2_AT
+Y_AT = W2_AT + 1024
+W1_AT = 8192
+PHI_COL_AT = W1_AT + 2048
+W1_BF_AT = 16384
+VW_AT = W1_BF_AT
 VW_TAB_AT = 20480
 W2_CODES_AT = VW_TAB_AT
 E_PIECES = ((0, 128), (128, 256), (256, 512))
@@ -49,13 +52,14 @@ def tile_picked_ymionet_val_p_kernel(
         placed = ctx.enter_context(tc.tile_pool(name="placed", bufs=1))
         ps = ctx.enter_context(tc.psum_pool(name="ps", bufs=1))
 
-        def scale_table(tile, engine):
-            engine.memset(tile[:].bitcast(I32), 0)
+        def load_scales(tile, scales):
+            nc.sync.dma_start(out=tile[0:P:SPREAD, :].bitcast(I32), in_=scales[0].bitcast(I32))
 
-        def load_scales(queues, tile, scales, row):
+        def place_scales(tile, picked, row):
             for r in range(4):
-                queues[r].dma_start(
-                    out=tile[row + r : P : QUADRANT, :].bitcast(I32), in_=scales[0, r:16:4, :].bitcast(I32)
+                nc.sync.dma_start(
+                    out=tile[row + r : P : QUADRANT, :].bitcast(I32),
+                    in_=picked[SPREAD * r : P : QUADRANT, :].bitcast(I32),
                 )
 
         def load_list(name, src):
@@ -69,44 +73,59 @@ def tile_picked_ymionet_val_p_kernel(
         def load_weight(tile, w):
             nc.sync.dma_start(out=tile[:], in_=w.rearrange("(p j) c -> p j c", j=PACK))
 
-        def cast_weight(copy, grouped, raw, h):
-            copy(
-                out=grouped[:].rearrange("p (r m j) -> p m j r", r=PACK, j=PACK)[:, :, :, 2 * h : 2 * h + 2],
-                in_=raw[:].rearrange("p j (m r) -> p m j r", r=PACK)[:, :, :, 2 * h : 2 * h + 2],
+        def cast_weight(grouped, raw, tiles):
+            nc.scalar.copy(
+                out=grouped[:].rearrange("p (r m j) -> p m j r", r=PACK, j=PACK)[:, :, :, tiles],
+                in_=raw[:].rearrange("p j (m r) -> p m j r", r=PACK)[:, :, :, tiles],
             )
 
         def quantize_weight(codes, scales, grouped):
             nc.vector.quantize_mx(out=codes.bitcast(FP8X4), scales=scales, in_=grouped)
 
         xs_tab = sb.tile([P, T], U8, name="xs_tab", align_bytes=ALIGN)
-        vs_tab = placed.tile([P, G], U8, name="vs_tab", align_bytes=ALIGN, offset=VS_TAB_AT)
+        vs_tab = sb.tile([P, G], U8, name="vs_tab", align_bytes=ALIGN)
         es_tab = sb.tile([P, W], U8, name="es_tab", align_bytes=ALIGN)
         xw_tab = sb.tile([P, T], I32, name="xw_tab", align_bytes=ALIGN)
         vw_tab = placed.tile([P, G], I32, name="vw_tab", align_bytes=ALIGN, offset=VW_TAB_AT)
         ew_tab = sb.tile([P, W], I32, name="ew_tab", align_bytes=ALIGN)
         phi_tab = sb.tile([P, G], F32, name="phi_tab")
-        scale_table(xs_tab, nc.gpsimd)
-        scale_table(vs_tab, nc.vector)
+        xs = sb.tile([P, S], U8, name="xs", align_bytes=ALIGN)
+        es = sb.tile([P, S], U8, name="es", align_bytes=ALIGN)
+        vs = sb.tile([P, V], U8, name="vs", align_bytes=ALIGN)
         nc.vector.memset(phi_tab[:], 0.0)
-        scale_table(es_tab, nc.gpsimd)
+        for tile in (xs_tab, es_tab, vs_tab, xs, es, vs):
+            nc.vector.memset(tile[:].bitcast(I32), 0)
 
         ident = sb.tile([P, P], F32, name="ident")
-        make_identity(nc, ident[:])
+        zero = sb.tile([P, 1], F32, name="zero")
+        nc.gpsimd.memset(zero[:], 0.0)
+        nc.scalar.copy(out=ident[:], in_=zero[:].to_broadcast([P, P]))
+        make_identity(nc, ident[:], nomemset=True)
 
-        offs_sb = load_list("offs_sb", offs)
         load_words(xw_tab, x_words)
-        load_scales([nc.scalar, nc.scalar, nc.sync, nc.sync], xs_tab, x_scales, X_ROW)
+        offs_sb = load_list("offs_sb", offs)
         pts_sb = load_list("pts_sb", pts)
-        w1_raw = sb.tile([P, PACK, H], F32, name="w1_raw", align_bytes=ALIGN)
-        load_weight(w1_raw, w1)
-        load_scales([nc.sync] * 4, vs_tab, v_scales, V_ROW)
         nc.sync.dma_start(out=phi_tab[0:1, :], in_=phi[0:1, :])
+        load_scales(xs_tab, x_scales)
+        w1_raw = placed.tile([P, PACK, H], F32, name="w1_raw", align_bytes=ALIGN, offset=W1_AT)
+        load_weight(w1_raw, w1)
+        coef_sb = load_list("coef_sb", coef)
+        load_scales(es_tab, e_scales)
+        load_scales(vs_tab, v_scales)
         w2_raw = placed.tile([P, PACK, H], F32, name="w2_raw", align_bytes=ALIGN, offset=W2_AT)
         load_weight(w2_raw, w2)
-        coef_sb = load_list("coef_sb", coef)
-        load_scales([nc.sync] * 4, es_tab, e_scales, E_ROW)
         load_words(vw_tab, v_words)
+
+        es_picked = sb.tile([P, S], U8, name="es_picked", align_bytes=ALIGN)
+        xs_picked = sb.tile([P, S], U8, name="xs_picked", align_bytes=ALIGN)
+        vs_picked = sb.tile([P, V], U8, name="vs_picked", align_bytes=ALIGN)
+        nc.vector.tensor_copy(xs_picked[:], xs_tab[:].indirect(offs_sb[:]))
+        nc.vector.tensor_copy(es_picked[:], es_tab[:].indirect(coef_sb[:]))
+        nc.vector.tensor_copy(vs_picked[:], vs_tab[:].indirect(pts_sb[:]))
+        place_scales(xs, xs_picked, X_ROW)
         load_words(ew_tab, e_words)
+        place_scales(es, es_picked, E_ROW)
+        place_scales(vs, vs_picked, V_ROW)
         lift_sb = [None] * CHUNKS
         for h in (FIRST // 2, THIRD // 2):
             tile = sb.tile([P, 2, V], F32, name="lift%d" % h)
@@ -114,32 +133,26 @@ def tile_picked_ymionet_val_p_kernel(
             for c in range(2):
                 lift_sb[2 * h + c] = tile[:, c, :]
 
-        xs = sb.tile([P, S], U8, name="xs", align_bytes=ALIGN)
-        es = sb.tile([P, S], U8, name="es", align_bytes=ALIGN)
-        vs = sb.tile([P, V], U8, name="vs", align_bytes=ALIGN)
         xw = sb.tile([P, S], U32, name="xw", align_bytes=ALIGN)
         phi_pts = sb.tile([P, V], F32, name="phi_pts")
-        w1_bf = sb.tile([P, H * PACK], BF16, name="w1_bf", align_bytes=ALIGN)
+        w1_bf = placed.tile([P, H * PACK], BF16, name="w1_bf", align_bytes=ALIGN, offset=W1_BF_AT)
         w2_bf = sb.tile([P, H * PACK], BF16, name="w2_bf", align_bytes=ALIGN)
-        w1_codes = placed.tile([P, H], U32, name="w1_codes", align_bytes=ALIGN, offset=W1_CODES_AT)
+        w1_codes = sb.tile([P, H], U32, name="w1_codes", align_bytes=ALIGN)
         w2_codes = placed.tile([P, H], U32, name="w2_codes", align_bytes=ALIGN, offset=W2_CODES_AT)
-        vw = sb.tile([P, V], U32, name="vw", align_bytes=ALIGN)
+        vw = placed.tile([P, V], U32, name="vw", align_bytes=ALIGN, offset=VW_AT)
         ew = sb.tile([P, S], U32, name="ew", align_bytes=ALIGN)
         w1_scales = sb.tile([P, H], U8, name="w1_scales", align_bytes=ALIGN)
         w2_scales = sb.tile([P, H], U8, name="w2_scales", align_bytes=ALIGN)
 
         nc.vector.tensor_copy(xw[:], xw_tab[:].bitcast(U32).indirect(offs_sb[:]))
-        nc.vector.tensor_copy(xs[:], xs_tab[:].indirect(offs_sb[:]))
-        cast_weight(nc.scalar.copy, w1_bf, w1_raw, 0)
-        cast_weight(nc.vector.tensor_copy, w1_bf, w1_raw, 1)
-        nc.vector.tensor_copy(vs[:], vs_tab[:].indirect(pts_sb[:]))
         nc.scalar.activation(phi_pts[:], phi_tab[:].indirect(pts_sb[:]), COPY)
+        cast_weight(w1_bf, w1_raw, slice(0, PACK))
         quantize_weight(w1_codes[:], w1_scales[:], w1_bf[:])
-        nc.vector.tensor_copy(es[:], es_tab[:].indirect(coef_sb[:]))
-        cast_weight(nc.scalar.copy, w2_bf, w2_raw, 0)
-        cast_weight(nc.scalar.copy, w2_bf, w2_raw, 1)
         nc.vector.tensor_copy(vw[:], vw_tab[:].bitcast(U32).indirect(pts_sb[:]))
-        quantize_weight(w2_codes[:], w2_scales[:], w2_bf[:])
+        for h in range(2):
+            cast_weight(w2_bf, w2_raw, slice(2 * h, 2 * h + 2))
+            places = slice(h * H // 2, (h + 1) * H // 2)
+            quantize_weight(w2_codes[:, places], w2_scales[:, places], w2_bf[:, 2 * h * H : 2 * (h + 1) * H])
 
         w1_tiles = [w1_codes[:, r * P : (r + 1) * P] for r in range(PACK)]
         w2_tiles = [w2_codes[:, r * P : (r + 1) * P] for r in range(PACK)]
@@ -162,6 +175,12 @@ def tile_picked_ymionet_val_p_kernel(
             nc.tensor.transpose(col_bank[:, b, :], phi_pts[:, b * P : (b + 1) * P], ident[:])
         phi_col = placed.tile([P, POINT_BLOCKS], F32, name="phi_col", align_bytes=ALIGN, offset=PHI_COL_AT)
         nc.scalar.copy(out=phi_col[:], in_=col_bank[:, :, 0])
+
+        row_bank = ps.tile([P, POINT_BLOCKS // 2, P], F32, name="row_bank", tag="b%d" % LAST)
+        for b in range(POINT_BLOCKS // 2):
+            nc.tensor.transpose(row_bank[:, b, :], phi_col[:, b : b + 1].to_broadcast([P, P]), ident[:])
+        phi_left = placed.tile([P, V // 2], F32, name="phi_left", align_bytes=ALIGN, offset=PHI_LEFT_AT)
+        nc.scalar.copy(out=phi_left[:], in_=row_bank[:].rearrange("p b v -> p (b v)"))
 
         y_sb = placed.tile([P, CHUNKS, P, PACK], F32, name="y_sb", align_bytes=ALIGN, offset=Y_AT)
         for c in (FIRST, SECOND, THIRD, LAST):
@@ -221,27 +240,37 @@ def tile_picked_ymionet_val_p_kernel(
             nc.sync.dma_start(out=out[c * P : (c + 1) * P, points], in_=result[c][:, points])
 
         whole, left, right = slice(0, V), slice(0, V // 2), slice(V // 2, V)
-        all_blocks = range(POINT_BLOCKS)
-        left_blocks, right_blocks = range(POINT_BLOCKS // 2), range(POINT_BLOCKS // 2, POINT_BLOCKS)
+        all_blocks, right_blocks = range(POINT_BLOCKS), range(POINT_BLOCKS // 2, POINT_BLOCKS)
         make_z(FIRST)
         make_z(SECOND)
         quantize_z(FIRST)
         product_turned(FIRST, all_blocks)
-        make_z(THIRD)
         quantize_z(SECOND)
         product_turned(SECOND, all_blocks)
+        make_z(THIRD)
         back_first = turn_back(FIRST, all_blocks, "b%d" % FIRST)
         make_z(LAST)
         quantize_z(THIRD)
         product_turned(THIRD, all_blocks)
         quantize_z(LAST)
-        product_turned(LAST, all_blocks)
+        plain_bank = ps.tile([P, V // 2], F32, name="plain_bank", tag="a%d" % FIRST)
+        nc.tensor.matmul_mx(
+            out=plain_bank[:],
+            lhsT=z_codes[LAST][:].bitcast(FP8X4),
+            lhsT_scale=z_scales[LAST][:],
+            rhs=vw[:, left].bitcast(FP8X4),
+            rhs_scale=vs[V_ROW:P, left],
+            start=True,
+            stop=True,
+        )
+        product_turned(LAST, right_blocks)
         back_second = turn_back(SECOND, all_blocks, "b%d" % SECOND)
         back_third = turn_back(THIRD, all_blocks, "b%d" % THIRD)
-        back_left = turn_back(LAST, left_blocks, "b%d" % LAST)
-        back_right = turn_back(LAST, right_blocks, "a%d" % FIRST)
+        back_last = turn_back(LAST, right_blocks, "b%d" % LAST)
         finish(FIRST, back_first[:], whole)
+        plain_scaled = sb.tile([P, V // 2], F32, name="plain_scaled")
+        nc.vector.tensor_tensor(plain_scaled[:], plain_bank[:], phi_left[:], MULT)
         finish(SECOND, back_second[:], whole)
+        finish(LAST, plain_scaled[:], left)
         finish(THIRD, back_third[:], whole)
-        finish(LAST, back_left[:, left], left)
-        finish(LAST, back_right[:, right], right)
+        finish(LAST, back_last[:, right], right)

@@ -20,15 +20,17 @@ COPY = mybir.ActivationFunctionType.Copy
 P = 128
 PACK = 4
 QUADRANT = 32
+SPREAD = 8
 LIST_ROWS = 16
 CHUNKS = S // P
 POINT_BLOCKS = V // P
-SPREAD = 8
 ALIGN = 64
 
 X_ROW, E_ROW, V_ROW = 0, 4, 8
 
-FIRST, SECOND, THIRD, LAST = 0, 1, 2, 3
+FIRST, SECOND, THIRD, LAST = range(CHUNKS)
+
+E_PIECES = ((0, P), (P, 2 * P), (2 * P, S))
 
 W2_AT = 0
 PHI_LEFT_AT = W2_AT
@@ -37,9 +39,6 @@ W1_AT = 8192
 PHI_COL_AT = W1_AT + 2048
 W1_BF_AT = 16384
 VW_AT = W1_BF_AT
-VW_TAB_AT = 20480
-W2_CODES_AT = VW_TAB_AT
-E_PIECES = ((0, 128), (128, 256), (256, 512))
 
 
 def tile_picked_ymionet_val_p_kernel(
@@ -70,8 +69,8 @@ def tile_picked_ymionet_val_p_kernel(
         def load_words(tile, words):
             nc.sync.dma_start(out=tile[:], in_=words[0].rearrange("p n t -> p (n t)").bitcast(I32))
 
-        def load_weight(tile, w):
-            nc.sync.dma_start(out=tile[:], in_=w.rearrange("(p j) c -> p j c", j=PACK))
+        def load_weight(tile, w, rows):
+            nc.sync.dma_start(out=tile[:, rows, :], in_=w.rearrange("(p j) c -> p j c", j=PACK)[:, rows, :])
 
         def cast_weight(grouped, raw, tiles):
             nc.scalar.copy(
@@ -86,14 +85,16 @@ def tile_picked_ymionet_val_p_kernel(
         vs_tab = sb.tile([P, G], U8, name="vs_tab", align_bytes=ALIGN)
         es_tab = sb.tile([P, W], U8, name="es_tab", align_bytes=ALIGN)
         xw_tab = sb.tile([P, T], I32, name="xw_tab", align_bytes=ALIGN)
-        vw_tab = placed.tile([P, G], I32, name="vw_tab", align_bytes=ALIGN, offset=VW_TAB_AT)
+        vw_tab = sb.tile([P, G], I32, name="vw_tab", align_bytes=ALIGN)
         ew_tab = sb.tile([P, W], I32, name="ew_tab", align_bytes=ALIGN)
         phi_tab = sb.tile([P, G], F32, name="phi_tab")
         xs = sb.tile([P, S], U8, name="xs", align_bytes=ALIGN)
         es = sb.tile([P, S], U8, name="es", align_bytes=ALIGN)
         vs = sb.tile([P, V], U8, name="vs", align_bytes=ALIGN)
+
+        nc.vector.memset(xs_tab[:].bitcast(I32), 0)
         nc.vector.memset(phi_tab[:], 0.0)
-        for tile in (xs_tab, es_tab, vs_tab, xs, es, vs):
+        for tile in (es_tab, vs_tab, xs, es, vs):
             nc.vector.memset(tile[:].bitcast(I32), 0)
 
         ident = sb.tile([P, P], F32, name="ident")
@@ -105,15 +106,16 @@ def tile_picked_ymionet_val_p_kernel(
         load_words(xw_tab, x_words)
         offs_sb = load_list("offs_sb", offs)
         pts_sb = load_list("pts_sb", pts)
-        nc.sync.dma_start(out=phi_tab[0:1, :], in_=phi[0:1, :])
         load_scales(xs_tab, x_scales)
         w1_raw = placed.tile([P, PACK, H], F32, name="w1_raw", align_bytes=ALIGN, offset=W1_AT)
-        load_weight(w1_raw, w1)
+        load_weight(w1_raw, w1, slice(0, 2))
+        nc.sync.dma_start(out=phi_tab[0:1, :], in_=phi[0:1, :])
+        load_weight(w1_raw, w1, slice(2, PACK))
         coef_sb = load_list("coef_sb", coef)
         load_scales(es_tab, e_scales)
         load_scales(vs_tab, v_scales)
         w2_raw = placed.tile([P, PACK, H], F32, name="w2_raw", align_bytes=ALIGN, offset=W2_AT)
-        load_weight(w2_raw, w2)
+        load_weight(w2_raw, w2, slice(0, PACK))
         load_words(vw_tab, v_words)
 
         es_picked = sb.tile([P, S], U8, name="es_picked", align_bytes=ALIGN)
@@ -126,19 +128,18 @@ def tile_picked_ymionet_val_p_kernel(
         load_words(ew_tab, e_words)
         place_scales(es, es_picked, E_ROW)
         place_scales(vs, vs_picked, V_ROW)
-        lift_sb = [None] * CHUNKS
-        for h in (FIRST // 2, THIRD // 2):
+        lift_sb = []
+        for h in range(2):
             tile = sb.tile([P, 2, V], F32, name="lift%d" % h)
             nc.sync.dma_start(out=tile[:], in_=lift[2 * P * h : 2 * P * (h + 1), :].rearrange("(c p) v -> p c v", p=P))
-            for c in range(2):
-                lift_sb[2 * h + c] = tile[:, c, :]
+            lift_sb.extend([tile[:, 0, :], tile[:, 1, :]])
 
         xw = sb.tile([P, S], U32, name="xw", align_bytes=ALIGN)
         phi_pts = sb.tile([P, V], F32, name="phi_pts")
         w1_bf = placed.tile([P, H * PACK], BF16, name="w1_bf", align_bytes=ALIGN, offset=W1_BF_AT)
         w2_bf = sb.tile([P, H * PACK], BF16, name="w2_bf", align_bytes=ALIGN)
         w1_codes = sb.tile([P, H], U32, name="w1_codes", align_bytes=ALIGN)
-        w2_codes = placed.tile([P, H], U32, name="w2_codes", align_bytes=ALIGN, offset=W2_CODES_AT)
+        w2_codes = sb.tile([P, H], U32, name="w2_codes", align_bytes=ALIGN)
         vw = placed.tile([P, V], U32, name="vw", align_bytes=ALIGN, offset=VW_AT)
         ew = sb.tile([P, S], U32, name="ew", align_bytes=ALIGN)
         w1_scales = sb.tile([P, H], U8, name="w1_scales", align_bytes=ALIGN)
@@ -154,15 +155,12 @@ def tile_picked_ymionet_val_p_kernel(
             places = slice(h * H // 2, (h + 1) * H // 2)
             quantize_weight(w2_codes[:, places], w2_scales[:, places], w2_bf[:, 2 * h * H : 2 * (h + 1) * H])
 
-        w1_tiles = [w1_codes[:, r * P : (r + 1) * P] for r in range(PACK)]
-        w2_tiles = [w2_codes[:, r * P : (r + 1) * P] for r in range(PACK)]
-
         def first_product(bank, codes, scales, words, word_scales):
             for r in range(PACK):
                 hid = slice(r * P, (r + 1) * P)
                 nc.tensor.matmul_mx(
                     out=bank[:, r, :],
-                    lhsT=codes[r].bitcast(FP8X4),
+                    lhsT=codes[:, hid].bitcast(FP8X4),
                     lhsT_scale=scales[:, hid],
                     rhs=words.bitcast(FP8X4),
                     rhs_scale=word_scales,
@@ -183,10 +181,10 @@ def tile_picked_ymionet_val_p_kernel(
         nc.scalar.copy(out=phi_left[:], in_=row_bank[:].rearrange("p b v -> p (b v)"))
 
         y_sb = placed.tile([P, CHUNKS, P, PACK], F32, name="y_sb", align_bytes=ALIGN, offset=Y_AT)
-        for c in (FIRST, SECOND, THIRD, LAST):
+        for c in range(CHUNKS):
             entries = slice(c * P, (c + 1) * P)
             bank = ps.tile([P, PACK, P], F32, name="y_bank%d" % c, tag="a%d" % c)
-            first_product(bank, w1_tiles, w1_scales, xw[:, entries], xs[X_ROW:P, entries])
+            first_product(bank, w1_codes, w1_scales, xw[:, entries], xs[X_ROW:P, entries])
             nc.scalar.copy(out=y_sb[:, c], in_=bank[:].rearrange("p r t -> p t r"))
 
         for start, stop in E_PIECES:
@@ -196,7 +194,7 @@ def tile_picked_ymionet_val_p_kernel(
         for c in range(CHUNKS):
             entries = slice(c * P, (c + 1) * P)
             bank = ps.tile([P, PACK, P], F32, name="e_bank%d" % c, tag="b%d" % c)
-            first_product(bank, w2_tiles, w2_scales, ew[:, entries], es[E_ROW:P, entries])
+            first_product(bank, w2_codes, w2_scales, ew[:, entries], es[E_ROW:P, entries])
             e_banks.append(bank)
 
         z_bf = [sb.tile([P, P, PACK], BF16, name="z_bf%d" % c, align_bytes=ALIGN) for c in range(CHUNKS)]
@@ -229,8 +227,8 @@ def tile_picked_ymionet_val_p_kernel(
             for b in blocks:
                 nc.scalar.activation(turned[c][:, b, :], bank[:, b, :], COPY, scale=phi_col[:, b : b + 1])
 
-        def turn_back(c, blocks, tag):
-            bank = ps.tile([P, V], F32, name="back_bank%d_%d" % (c, blocks.start), tag=tag)
+        def turn_back(c, blocks):
+            bank = ps.tile([P, V], F32, name="back_bank%d" % c, tag="b%d" % c)
             for b in blocks:
                 nc.tensor.transpose(bank[:, b * P : (b + 1) * P], turned[c][:, b, :], ident[:])
             return bank
@@ -248,7 +246,7 @@ def tile_picked_ymionet_val_p_kernel(
         quantize_z(SECOND)
         product_turned(SECOND, all_blocks)
         make_z(THIRD)
-        back_first = turn_back(FIRST, all_blocks, "b%d" % FIRST)
+        back_first = turn_back(FIRST, all_blocks)
         make_z(LAST)
         quantize_z(THIRD)
         product_turned(THIRD, all_blocks)
@@ -264,9 +262,9 @@ def tile_picked_ymionet_val_p_kernel(
             stop=True,
         )
         product_turned(LAST, right_blocks)
-        back_second = turn_back(SECOND, all_blocks, "b%d" % SECOND)
-        back_third = turn_back(THIRD, all_blocks, "b%d" % THIRD)
-        back_last = turn_back(LAST, right_blocks, "b%d" % LAST)
+        back_second = turn_back(SECOND, all_blocks)
+        back_third = turn_back(THIRD, all_blocks)
+        back_last = turn_back(LAST, right_blocks)
         finish(FIRST, back_first[:], whole)
         plain_scaled = sb.tile([P, V // 2], F32, name="plain_scaled")
         nc.vector.tensor_tensor(plain_scaled[:], plain_bank[:], phi_left[:], MULT)

@@ -33,10 +33,9 @@ FIRST, SECOND, THIRD, LAST = range(CHUNKS)
 E_PIECES = ((0, P), (P, 2 * P), (2 * P, S))
 
 W2_AT = 0
-PHI_LEFT_AT = W2_AT
-Y_AT = W2_AT + 1024
+Y_AT = W2_AT
 W1_AT = 8192
-PHI_COL_AT = W1_AT + 2048
+PHI_COL_AT = W1_AT
 W1_BF_AT = 16384
 VW_AT = W1_BF_AT
 
@@ -174,12 +173,6 @@ def tile_picked_ymionet_val_p_kernel(
         phi_col = placed.tile([P, POINT_BLOCKS], F32, name="phi_col", align_bytes=ALIGN, offset=PHI_COL_AT)
         nc.scalar.copy(out=phi_col[:], in_=col_bank[:, :, 0])
 
-        row_bank = ps.tile([P, POINT_BLOCKS // 2, P], F32, name="row_bank", tag="b%d" % LAST)
-        for b in range(POINT_BLOCKS // 2):
-            nc.tensor.transpose(row_bank[:, b, :], phi_col[:, b : b + 1].to_broadcast([P, P]), ident[:])
-        phi_left = placed.tile([P, V // 2], F32, name="phi_left", align_bytes=ALIGN, offset=PHI_LEFT_AT)
-        nc.scalar.copy(out=phi_left[:], in_=row_bank[:].rearrange("p b v -> p (b v)"))
-
         y_sb = placed.tile([P, CHUNKS, P, PACK], F32, name="y_sb", align_bytes=ALIGN, offset=Y_AT)
         for c in range(CHUNKS):
             entries = slice(c * P, (c + 1) * P)
@@ -227,8 +220,8 @@ def tile_picked_ymionet_val_p_kernel(
             for b in blocks:
                 nc.scalar.activation(turned[c][:, b, :], bank[:, b, :], COPY, scale=phi_col[:, b : b + 1])
 
-        def turn_back(c, blocks):
-            bank = ps.tile([P, V], F32, name="back_bank%d" % c, tag="b%d" % c)
+        def turn_back(c, blocks, tag):
+            bank = ps.tile([P, V], F32, name="back_bank%d_%d" % (c, blocks.start), tag=tag)
             for b in blocks:
                 nc.tensor.transpose(bank[:, b * P : (b + 1) * P], turned[c][:, b, :], ident[:])
             return bank
@@ -238,7 +231,8 @@ def tile_picked_ymionet_val_p_kernel(
             nc.sync.dma_start(out=out[c * P : (c + 1) * P, points], in_=result[c][:, points])
 
         whole, left, right = slice(0, V), slice(0, V // 2), slice(V // 2, V)
-        all_blocks, right_blocks = range(POINT_BLOCKS), range(POINT_BLOCKS // 2, POINT_BLOCKS)
+        all_blocks = range(POINT_BLOCKS)
+        left_blocks, right_blocks = range(POINT_BLOCKS // 2), range(POINT_BLOCKS // 2, POINT_BLOCKS)
         make_z(FIRST)
         make_z(SECOND)
         quantize_z(FIRST)
@@ -246,29 +240,18 @@ def tile_picked_ymionet_val_p_kernel(
         quantize_z(SECOND)
         product_turned(SECOND, all_blocks)
         make_z(THIRD)
-        back_first = turn_back(FIRST, all_blocks)
+        back_first = turn_back(FIRST, all_blocks, "b%d" % FIRST)
         make_z(LAST)
         quantize_z(THIRD)
         product_turned(THIRD, all_blocks)
         quantize_z(LAST)
-        plain_bank = ps.tile([P, V // 2], F32, name="plain_bank", tag="a%d" % FIRST)
-        nc.tensor.matmul_mx(
-            out=plain_bank[:],
-            lhsT=z_codes[LAST][:].bitcast(FP8X4),
-            lhsT_scale=z_scales[LAST][:],
-            rhs=vw[:, left].bitcast(FP8X4),
-            rhs_scale=vs[V_ROW:P, left],
-            start=True,
-            stop=True,
-        )
-        product_turned(LAST, right_blocks)
-        back_second = turn_back(SECOND, all_blocks)
-        back_third = turn_back(THIRD, all_blocks)
-        back_last = turn_back(LAST, right_blocks)
+        product_turned(LAST, all_blocks)
+        back_second = turn_back(SECOND, all_blocks, "b%d" % SECOND)
+        back_third = turn_back(THIRD, all_blocks, "b%d" % THIRD)
+        back_left = turn_back(LAST, left_blocks, "b%d" % LAST)
+        back_right = turn_back(LAST, right_blocks, "a%d" % FIRST)
         finish(FIRST, back_first[:], whole)
-        plain_scaled = sb.tile([P, V // 2], F32, name="plain_scaled")
-        nc.vector.tensor_tensor(plain_scaled[:], plain_bank[:], phi_left[:], MULT)
         finish(SECOND, back_second[:], whole)
-        finish(LAST, plain_scaled[:], left)
         finish(THIRD, back_third[:], whole)
-        finish(LAST, back_last[:, right], right)
+        finish(LAST, back_left[:, left], left)
+        finish(LAST, back_right[:, right], right)

@@ -26,7 +26,7 @@ CHUNKS = S // P
 POINT_BLOCKS = V // P
 ALIGN = 64
 
-X_ROW, E_ROW, V_ROW = 0, 4, 8
+X_AT, E_AT = 0, S
 
 FIRST, SECOND, THIRD, LAST = range(CHUNKS)
 
@@ -34,10 +34,12 @@ E_PIECES = ((0, P), (P, 2 * P), (2 * P, S))
 
 W2_AT = 0
 Y_AT = W2_AT
-W1_AT = 8192
-PHI_COL_AT = W1_AT
-W1_BF_AT = 16384
+W1_BF_AT = 8192
 VW_AT = W1_BF_AT
+EW_TAB_AT = 12288
+LIFT_AT = EW_TAB_AT + 8192
+ES_TAB_AT = EW_TAB_AT
+VS_TAB_AT = LIFT_AT
 
 
 def tile_picked_ymionet_val_p_kernel(
@@ -53,13 +55,6 @@ def tile_picked_ymionet_val_p_kernel(
         def load_scales(tile, scales):
             nc.sync.dma_start(out=tile[0:P:SPREAD, :].bitcast(I32), in_=scales[0].bitcast(I32))
 
-        def place_scales(tile, picked, row):
-            for r in range(4):
-                nc.sync.dma_start(
-                    out=tile[row + r : P : QUADRANT, :].bitcast(I32),
-                    in_=picked[SPREAD * r : P : QUADRANT, :].bitcast(I32),
-                )
-
         def load_list(name, src):
             tile = lists.tile([P, S // LIST_ROWS], U16, name=name)
             nc.sync.dma_start(tile[:], src)
@@ -68,33 +63,49 @@ def tile_picked_ymionet_val_p_kernel(
         def load_words(tile, words):
             nc.sync.dma_start(out=tile[:], in_=words[0].rearrange("p n t -> p (n t)").bitcast(I32))
 
-        def load_weight(tile, w, rows):
-            nc.sync.dma_start(out=tile[:, rows, :], in_=w.rearrange("(p j) c -> p j c", j=PACK)[:, rows, :])
+        def load_weight(tile, w):
+            nc.sync.dma_start(out=tile[:], in_=w.rearrange("(p j) c -> p j c", j=PACK))
 
-        def cast_weight(grouped, raw, tiles):
-            nc.scalar.copy(
-                out=grouped[:].rearrange("p (r m j) -> p m j r", r=PACK, j=PACK)[:, :, :, tiles],
-                in_=raw[:].rearrange("p j (m r) -> p m j r", r=PACK)[:, :, :, tiles],
+        def place_scales(planes, picked):
+            for r in range(4):
+                nc.sync.dma_start(
+                    out=planes[r:P:QUADRANT, :].bitcast(I32), in_=picked[SPREAD * r : P : QUADRANT, :].bitcast(I32)
+                )
+
+        def cast_views(grouped, raw, places, tiles):
+            return (
+                grouped[:].rearrange("p (r m j) -> p m j r", r=PACK, j=PACK)[:, places, :, tiles],
+                raw[:].rearrange("p j (m r) -> p m j r", r=PACK)[:, places, :, tiles],
             )
 
-        def quantize_weight(codes, scales, grouped):
-            nc.vector.quantize_mx(out=codes.bitcast(FP8X4), scales=scales, in_=grouped)
-
         xs_tab = sb.tile([P, T], U8, name="xs_tab", align_bytes=ALIGN)
-        vs_tab = sb.tile([P, G], U8, name="vs_tab", align_bytes=ALIGN)
-        es_tab = sb.tile([P, W], U8, name="es_tab", align_bytes=ALIGN)
+        vs_tab = placed.tile([P, G], U8, name="vs_tab", align_bytes=ALIGN, offset=VS_TAB_AT)
+        es_tab = placed.tile([P, W], U8, name="es_tab", align_bytes=ALIGN, offset=ES_TAB_AT)
         xw_tab = sb.tile([P, T], I32, name="xw_tab", align_bytes=ALIGN)
         vw_tab = sb.tile([P, G], I32, name="vw_tab", align_bytes=ALIGN)
-        ew_tab = sb.tile([P, W], I32, name="ew_tab", align_bytes=ALIGN)
         phi_tab = sb.tile([P, G], F32, name="phi_tab")
-        xs = sb.tile([P, S], U8, name="xs", align_bytes=ALIGN)
-        es = sb.tile([P, S], U8, name="es", align_bytes=ALIGN)
-        vs = sb.tile([P, V], U8, name="vs", align_bytes=ALIGN)
+        xe_picked = sb.tile([P, 2 * S], U8, name="xe_picked", align_bytes=ALIGN)
+        xe_planes = sb.tile([P, 2 * S], U8, name="xe_planes", align_bytes=ALIGN)
+        v_picked = sb.tile([P, V], U8, name="v_picked", align_bytes=ALIGN)
+        v_plane = sb.tile([P, V], U8, name="v_plane", align_bytes=ALIGN)
 
-        nc.vector.memset(xs_tab[:].bitcast(I32), 0)
         nc.vector.memset(phi_tab[:], 0.0)
-        for tile in (es_tab, vs_tab, xs, es, vs):
+        for tile in (xs_tab, es_tab, vs_tab, xe_planes, v_plane):
             nc.vector.memset(tile[:].bitcast(I32), 0)
+
+        load_words(xw_tab, x_words)
+        offs_sb = load_list("offs_sb", offs)
+        pts_sb = load_list("pts_sb", pts)
+        coef_sb = load_list("coef_sb", coef)
+        nc.sync.dma_start(out=phi_tab[0:1, :], in_=phi[0:1, :])
+        load_scales(xs_tab, x_scales)
+        load_scales(es_tab, e_scales)
+        w1_raw = sb.tile([P, PACK, H], F32, name="w1_raw", align_bytes=ALIGN)
+        load_weight(w1_raw, w1)
+        load_scales(vs_tab, v_scales)
+        w2_raw = placed.tile([P, PACK, H], F32, name="w2_raw", align_bytes=ALIGN, offset=W2_AT)
+        load_weight(w2_raw, w2)
+        load_words(vw_tab, v_words)
 
         ident = sb.tile([P, P], F32, name="ident")
         zero = sb.tile([P, 1], F32, name="zero")
@@ -102,38 +113,19 @@ def tile_picked_ymionet_val_p_kernel(
         nc.scalar.copy(out=ident[:], in_=zero[:].to_broadcast([P, P]))
         make_identity(nc, ident[:], nomemset=True)
 
-        load_words(xw_tab, x_words)
-        offs_sb = load_list("offs_sb", offs)
-        pts_sb = load_list("pts_sb", pts)
-        load_scales(xs_tab, x_scales)
-        w1_raw = placed.tile([P, PACK, H], F32, name="w1_raw", align_bytes=ALIGN, offset=W1_AT)
-        load_weight(w1_raw, w1, slice(0, 2))
-        nc.sync.dma_start(out=phi_tab[0:1, :], in_=phi[0:1, :])
-        load_weight(w1_raw, w1, slice(2, PACK))
-        coef_sb = load_list("coef_sb", coef)
-        load_scales(es_tab, e_scales)
-        load_scales(vs_tab, v_scales)
-        w2_raw = placed.tile([P, PACK, H], F32, name="w2_raw", align_bytes=ALIGN, offset=W2_AT)
-        load_weight(w2_raw, w2, slice(0, PACK))
-        load_words(vw_tab, v_words)
-
-        es_picked = sb.tile([P, S], U8, name="es_picked", align_bytes=ALIGN)
-        xs_picked = sb.tile([P, S], U8, name="xs_picked", align_bytes=ALIGN)
-        vs_picked = sb.tile([P, V], U8, name="vs_picked", align_bytes=ALIGN)
-        nc.vector.tensor_copy(xs_picked[:], xs_tab[:].indirect(offs_sb[:]))
-        nc.vector.tensor_copy(es_picked[:], es_tab[:].indirect(coef_sb[:]))
-        nc.vector.tensor_copy(vs_picked[:], vs_tab[:].indirect(pts_sb[:]))
-        place_scales(xs, xs_picked, X_ROW)
+        nc.vector.tensor_copy(xe_picked[:, X_AT : X_AT + S], xs_tab[:].indirect(offs_sb[:]))
+        nc.vector.tensor_copy(xe_picked[:, E_AT : E_AT + S], es_tab[:].indirect(coef_sb[:]))
+        place_scales(xe_planes, xe_picked)
+        ew_tab = placed.tile([P, W], I32, name="ew_tab", align_bytes=ALIGN, offset=EW_TAB_AT)
         load_words(ew_tab, e_words)
-        place_scales(es, es_picked, E_ROW)
-        place_scales(vs, vs_picked, V_ROW)
-        lift_sb = []
-        for h in range(2):
-            tile = sb.tile([P, 2, V], F32, name="lift%d" % h)
-            nc.sync.dma_start(out=tile[:], in_=lift[2 * P * h : 2 * P * (h + 1), :].rearrange("(c p) v -> p c v", p=P))
-            lift_sb.extend([tile[:, 0, :], tile[:, 1, :]])
-
         xw = sb.tile([P, S], U32, name="xw", align_bytes=ALIGN)
+        nc.vector.tensor_copy(xw[:], xw_tab[:].bitcast(U32).indirect(offs_sb[:]))
+        nc.vector.tensor_copy(v_picked[:], vs_tab[:].indirect(pts_sb[:]))
+        place_scales(v_plane, v_picked)
+        lift_sb = placed.tile([P, CHUNKS, V], F32, name="lift_sb", align_bytes=ALIGN, offset=LIFT_AT)
+        for c in range(CHUNKS):
+            nc.sync.dma_start(out=lift_sb[:, c, :], in_=lift[c * P : (c + 1) * P, :])
+
         phi_pts = sb.tile([P, V], F32, name="phi_pts")
         w1_bf = placed.tile([P, H * PACK], BF16, name="w1_bf", align_bytes=ALIGN, offset=W1_BF_AT)
         w2_bf = sb.tile([P, H * PACK], BF16, name="w2_bf", align_bytes=ALIGN)
@@ -144,15 +136,20 @@ def tile_picked_ymionet_val_p_kernel(
         w1_scales = sb.tile([P, H], U8, name="w1_scales", align_bytes=ALIGN)
         w2_scales = sb.tile([P, H], U8, name="w2_scales", align_bytes=ALIGN)
 
-        nc.vector.tensor_copy(xw[:], xw_tab[:].bitcast(U32).indirect(offs_sb[:]))
         nc.scalar.activation(phi_pts[:], phi_tab[:].indirect(pts_sb[:]), COPY)
-        cast_weight(w1_bf, w1_raw, slice(0, PACK))
-        quantize_weight(w1_codes[:], w1_scales[:], w1_bf[:])
+        nc.scalar.copy(*cast_views(w1_bf, w1_raw, slice(0, P), slice(0, PACK)))
+        nc.vector.tensor_copy(*cast_views(w2_bf, w2_raw, slice(0, P // 2), slice(2, PACK)))
+        nc.scalar.copy(*cast_views(w2_bf, w2_raw, slice(0, P), slice(0, 2)))
+        nc.scalar.copy(*cast_views(w2_bf, w2_raw, slice(P // 2, P), slice(2, PACK)))
+        nc.vector.quantize_mx(out=w1_codes[:].bitcast(FP8X4), scales=w1_scales[:], in_=w1_bf[:])
         nc.vector.tensor_copy(vw[:], vw_tab[:].bitcast(U32).indirect(pts_sb[:]))
         for h in range(2):
-            cast_weight(w2_bf, w2_raw, slice(2 * h, 2 * h + 2))
             places = slice(h * H // 2, (h + 1) * H // 2)
-            quantize_weight(w2_codes[:, places], w2_scales[:, places], w2_bf[:, 2 * h * H : 2 * (h + 1) * H])
+            nc.vector.quantize_mx(
+                out=w2_codes[:, places].bitcast(FP8X4),
+                scales=w2_scales[:, places],
+                in_=w2_bf[:, 2 * h * H : 2 * (h + 1) * H],
+            )
 
         def first_product(bank, codes, scales, words, word_scales):
             for r in range(PACK):
@@ -167,17 +164,16 @@ def tile_picked_ymionet_val_p_kernel(
                     stop=True,
                 )
 
-        col_bank = ps.tile([P, POINT_BLOCKS, P], F32, name="col_bank", tag="a%d" % LAST)
+        col_bank = ps.tile([P, POINT_BLOCKS, P], F32, name="col_bank", tag="b2")
         for b in range(POINT_BLOCKS):
             nc.tensor.transpose(col_bank[:, b, :], phi_pts[:, b * P : (b + 1) * P], ident[:])
-        phi_col = placed.tile([P, POINT_BLOCKS], F32, name="phi_col", align_bytes=ALIGN, offset=PHI_COL_AT)
+        phi_col = sb.tile([P, POINT_BLOCKS], F32, name="phi_col")
         nc.scalar.copy(out=phi_col[:], in_=col_bank[:, :, 0])
 
         y_sb = placed.tile([P, CHUNKS, P, PACK], F32, name="y_sb", align_bytes=ALIGN, offset=Y_AT)
         for c in range(CHUNKS):
-            entries = slice(c * P, (c + 1) * P)
             bank = ps.tile([P, PACK, P], F32, name="y_bank%d" % c, tag="a%d" % c)
-            first_product(bank, w1_codes, w1_scales, xw[:, entries], xs[X_ROW:P, entries])
+            first_product(bank, w1_codes, w1_scales, xw[:, c * P : (c + 1) * P], xe_planes[:, X_AT + c * P : X_AT + (c + 1) * P])
             nc.scalar.copy(out=y_sb[:, c], in_=bank[:].rearrange("p r t -> p t r"))
 
         for start, stop in E_PIECES:
@@ -185,9 +181,8 @@ def tile_picked_ymionet_val_p_kernel(
             nc.vector.tensor_copy(ew[:, start:stop], ew_tab[:].bitcast(U32).indirect(offsets))
         e_banks = []
         for c in range(CHUNKS):
-            entries = slice(c * P, (c + 1) * P)
             bank = ps.tile([P, PACK, P], F32, name="e_bank%d" % c, tag="b%d" % c)
-            first_product(bank, w2_codes, w2_scales, ew[:, entries], es[E_ROW:P, entries])
+            first_product(bank, w2_codes, w2_scales, ew[:, c * P : (c + 1) * P], xe_planes[:, E_AT + c * P : E_AT + (c + 1) * P])
             e_banks.append(bank)
 
         z_bf = [sb.tile([P, P, PACK], BF16, name="z_bf%d" % c, align_bytes=ALIGN) for c in range(CHUNKS)]
@@ -195,6 +190,9 @@ def tile_picked_ymionet_val_p_kernel(
         z_scales = [sb.tile([P, P], U8, name="z_scales%d" % c, align_bytes=ALIGN) for c in range(CHUNKS)]
         turned = [sb.tile([P, POINT_BLOCKS, P], F32, name="turned%d" % c) for c in range(CHUNKS)]
         result = [sb.tile([P, V], F32, name="result%d" % c) for c in range(CHUNKS)]
+
+        def cols(blocks):
+            return slice(blocks.start * P, blocks.stop * P)
 
         def make_z(c):
             nc.vector.tensor_tensor(z_bf[c][:], e_banks[c][:].rearrange("p r t -> p t r"), y_sb[:, c], MULT)
@@ -204,14 +202,13 @@ def tile_picked_ymionet_val_p_kernel(
                 out=z_codes[c][:].bitcast(FP8X4), scales=z_scales[c][:], in_=z_bf[c][:].rearrange("p t r -> p (t r)")
             )
 
-        def product_turned(c, blocks):
-            bank = ps.tile([P, POINT_BLOCKS, P], F32, name="turned_bank%d" % c, tag="a%d" % c)
+        def product_turned(c, blocks, tag):
+            bank = ps.tile([P, POINT_BLOCKS, P], F32, name="turned_bank%d_%d" % (c, blocks.start), tag=tag)
             for b in blocks:
-                points = slice(b * P, (b + 1) * P)
                 nc.tensor.matmul_mx(
                     out=bank[:, b, :],
-                    lhsT=vw[:, points].bitcast(FP8X4),
-                    lhsT_scale=vs[V_ROW:P, points],
+                    lhsT=vw[:, b * P : (b + 1) * P].bitcast(FP8X4),
+                    lhsT_scale=v_plane[:, b * P : (b + 1) * P],
                     rhs=z_codes[c][:].bitcast(FP8X4),
                     rhs_scale=z_scales[c][:],
                     start=True,
@@ -220,38 +217,50 @@ def tile_picked_ymionet_val_p_kernel(
             for b in blocks:
                 nc.scalar.activation(turned[c][:, b, :], bank[:, b, :], COPY, scale=phi_col[:, b : b + 1])
 
+        def turn(bank, src, blocks, opens, closes):
+            for b in blocks:
+                nc.tensor.matmul(
+                    bank[:, b * P : (b + 1) * P],
+                    src[:, b, :],
+                    ident[:],
+                    start=opens and b == blocks[0],
+                    stop=closes and b == blocks[-1],
+                    is_transpose=True,
+                )
+
         def turn_back(c, blocks, tag):
             bank = ps.tile([P, V], F32, name="back_bank%d_%d" % (c, blocks.start), tag=tag)
-            for b in blocks:
-                nc.tensor.transpose(bank[:, b * P : (b + 1) * P], turned[c][:, b, :], ident[:])
+            turn(bank, turned[c], blocks, True, True)
             return bank
 
-        def finish(c, scaled, points):
-            nc.vector.tensor_tensor(result[c][:, points], scaled, lift_sb[c][:, points], ADD)
-            nc.sync.dma_start(out=out[c * P : (c + 1) * P, points], in_=result[c][:, points])
+        def store(c, blocks):
+            nc.sync.dma_start(out=out[c * P : (c + 1) * P, cols(blocks)], in_=result[c][:, cols(blocks)])
 
-        whole, left, right = slice(0, V), slice(0, V // 2), slice(V // 2, V)
-        all_blocks = range(POINT_BLOCKS)
-        left_blocks, right_blocks = range(POINT_BLOCKS // 2), range(POINT_BLOCKS // 2, POINT_BLOCKS)
+        def add_lift(c, src, blocks):
+            nc.vector.tensor_tensor(result[c][:, cols(blocks)], src[:, cols(blocks)], lift_sb[:, c, cols(blocks)], ADD)
+            store(c, blocks)
+
+        whole, left, right = range(POINT_BLOCKS), range(POINT_BLOCKS // 2), range(POINT_BLOCKS // 2, POINT_BLOCKS)
+
         make_z(FIRST)
         make_z(SECOND)
         quantize_z(FIRST)
-        product_turned(FIRST, all_blocks)
+        product_turned(FIRST, whole, "a0")
         quantize_z(SECOND)
-        product_turned(SECOND, all_blocks)
+        product_turned(SECOND, whole, "a1")
         make_z(THIRD)
-        back_first = turn_back(FIRST, all_blocks, "b%d" % FIRST)
+        back_first = turn_back(FIRST, whole, "b0")
         make_z(LAST)
         quantize_z(THIRD)
-        product_turned(THIRD, all_blocks)
+        product_turned(THIRD, whole, "a2")
         quantize_z(LAST)
-        product_turned(LAST, all_blocks)
-        back_second = turn_back(SECOND, all_blocks, "b%d" % SECOND)
-        back_third = turn_back(THIRD, all_blocks, "b%d" % THIRD)
-        back_left = turn_back(LAST, left_blocks, "b%d" % LAST)
-        back_right = turn_back(LAST, right_blocks, "a%d" % FIRST)
-        finish(FIRST, back_first[:], whole)
-        finish(SECOND, back_second[:], whole)
-        finish(THIRD, back_third[:], whole)
-        finish(LAST, back_left[:, left], left)
-        finish(LAST, back_right[:, right], right)
+        product_turned(LAST, whole, "a3")
+        back_second = turn_back(SECOND, whole, "b1")
+        back_third = turn_back(THIRD, whole, "b2")
+        back_left = turn_back(LAST, left, "b3")
+        back_right = turn_back(LAST, right, "a0")
+        add_lift(FIRST, back_first, whole)
+        add_lift(SECOND, back_second, whole)
+        add_lift(THIRD, back_third, whole)
+        add_lift(LAST, back_left, left)
+        add_lift(LAST, back_right, right)

@@ -194,8 +194,10 @@ def tile_picked_ymionet_val_p_kernel(
         def cols(blocks):
             return slice(blocks.start * P, blocks.stop * P)
 
-        def make_z(c):
-            nc.vector.tensor_tensor(z_bf[c][:], e_banks[c][:].rearrange("p r t -> p t r"), y_sb[:, c], MULT)
+        def make_z(c, entries):
+            nc.vector.tensor_tensor(
+                z_bf[c][:, entries, :], e_banks[c][:].rearrange("p r t -> p t r")[:, entries, :], y_sb[:, c, entries, :], MULT
+            )
 
         def quantize_z(c):
             nc.vector.quantize_mx(
@@ -242,25 +244,39 @@ def tile_picked_ymionet_val_p_kernel(
 
         whole, left, right = range(POINT_BLOCKS), range(POINT_BLOCKS // 2), range(POINT_BLOCKS // 2, POINT_BLOCKS)
 
-        make_z(FIRST)
-        make_z(SECOND)
+        early, late = slice(0, P // 2), slice(P // 2, P)
+        make_z(FIRST, slice(0, P))
+        make_z(SECOND, early)
         quantize_z(FIRST)
-        product_turned(FIRST, whole, "a0")
+        product_turned(FIRST, left, "a0")
+        product_turned(FIRST, right, "a1")
+        make_z(SECOND, late)
+        make_z(THIRD, early)
         quantize_z(SECOND)
-        product_turned(SECOND, whole, "a1")
-        make_z(THIRD)
-        back_first = turn_back(FIRST, whole, "b0")
-        make_z(LAST)
+        back_0l = turn_back(FIRST, left, "b0")
+        product_turned(SECOND, left, "a2")
+        product_turned(SECOND, right, "a3")
+        back_0r = turn_back(FIRST, right, "b1")
+        make_z(THIRD, late)
+        make_z(LAST, early)
         quantize_z(THIRD)
-        product_turned(THIRD, whole, "a2")
+        product_turned(THIRD, left, "a0")
+        product_turned(THIRD, right, "a1")
+        back_1l = turn_back(SECOND, left, "b2")
+        back_1r = turn_back(SECOND, right, "a2")
+        make_z(LAST, late)
+        add_lift(FIRST, back_0l, left)
         quantize_z(LAST)
-        product_turned(LAST, whole, "a3")
-        back_second = turn_back(SECOND, whole, "b1")
-        back_third = turn_back(THIRD, whole, "b2")
-        back_left = turn_back(LAST, left, "b3")
-        back_right = turn_back(LAST, right, "a0")
-        add_lift(FIRST, back_first, whole)
-        add_lift(SECOND, back_second, whole)
-        add_lift(THIRD, back_third, whole)
-        add_lift(LAST, back_left, left)
-        add_lift(LAST, back_right, right)
+        product_turned(LAST, left, "a3")
+        product_turned(LAST, right, "b3")
+        add_lift(FIRST, back_0r, right)
+        back_2l = turn_back(THIRD, left, "b0")
+        back_2r = turn_back(THIRD, right, "b1")
+        add_lift(SECOND, back_1l, left)
+        add_lift(SECOND, back_1r, right)
+        back_3l = turn_back(LAST, left, "a0")
+        back_3r = turn_back(LAST, right, "a1")
+        add_lift(THIRD, back_2l, left)
+        add_lift(THIRD, back_2r, right)
+        add_lift(LAST, back_3l, left)
+        add_lift(LAST, back_3r, right)

@@ -26,8 +26,6 @@ CHUNKS = S // P
 POINT_BLOCKS = V // P
 ALIGN = 64
 
-X_AT, E_AT = 0, S
-
 FIRST, SECOND, THIRD, LAST = range(CHUNKS)
 
 E_PIECES = ((0, P), (P, 2 * P), (2 * P, S))
@@ -38,8 +36,8 @@ W1_BF_AT = 8192
 VW_AT = W1_BF_AT
 EW_TAB_AT = 12288
 LIFT_AT = EW_TAB_AT + 8192
-ES_TAB_AT = EW_TAB_AT
-VS_TAB_AT = LIFT_AT
+VS_TAB_AT = EW_TAB_AT
+ES_TAB_AT = LIFT_AT
 
 
 def tile_picked_ymionet_val_p_kernel(
@@ -84,13 +82,14 @@ def tile_picked_ymionet_val_p_kernel(
         xw_tab = sb.tile([P, T], I32, name="xw_tab", align_bytes=ALIGN)
         vw_tab = sb.tile([P, G], I32, name="vw_tab", align_bytes=ALIGN)
         phi_tab = sb.tile([P, G], F32, name="phi_tab")
-        xe_picked = sb.tile([P, 2 * S], U8, name="xe_picked", align_bytes=ALIGN)
-        xe_planes = sb.tile([P, 2 * S], U8, name="xe_planes", align_bytes=ALIGN)
-        v_picked = sb.tile([P, V], U8, name="v_picked", align_bytes=ALIGN)
-        v_plane = sb.tile([P, V], U8, name="v_plane", align_bytes=ALIGN)
+        xv_picked = sb.tile([P, S + V], U8, name="xv_picked", align_bytes=ALIGN)
+        xv_planes = sb.tile([P, S + V], U8, name="xv_planes", align_bytes=ALIGN)
+        e_picked = sb.tile([P, S], U8, name="e_picked", align_bytes=ALIGN)
+        e_plane = sb.tile([P, S], U8, name="e_plane", align_bytes=ALIGN)
+        x_plane, v_plane = xv_planes[:, 0:S], xv_planes[:, S : S + V]
 
         nc.vector.memset(phi_tab[:], 0.0)
-        for tile in (xs_tab, es_tab, vs_tab, xe_planes, v_plane):
+        for tile in (xs_tab, vs_tab, es_tab, xv_planes, e_plane):
             nc.vector.memset(tile[:].bitcast(I32), 0)
 
         load_words(xw_tab, x_words)
@@ -99,10 +98,10 @@ def tile_picked_ymionet_val_p_kernel(
         coef_sb = load_list("coef_sb", coef)
         nc.sync.dma_start(out=phi_tab[0:1, :], in_=phi[0:1, :])
         load_scales(xs_tab, x_scales)
-        load_scales(es_tab, e_scales)
+        load_scales(vs_tab, v_scales)
         w1_raw = sb.tile([P, PACK, H], F32, name="w1_raw", align_bytes=ALIGN)
         load_weight(w1_raw, w1)
-        load_scales(vs_tab, v_scales)
+        load_scales(es_tab, e_scales)
         w2_raw = placed.tile([P, PACK, H], F32, name="w2_raw", align_bytes=ALIGN, offset=W2_AT)
         load_weight(w2_raw, w2)
         load_words(vw_tab, v_words)
@@ -113,15 +112,15 @@ def tile_picked_ymionet_val_p_kernel(
         nc.scalar.copy(out=ident[:], in_=zero[:].to_broadcast([P, P]))
         make_identity(nc, ident[:], nomemset=True)
 
-        nc.vector.tensor_copy(xe_picked[:, X_AT : X_AT + S], xs_tab[:].indirect(offs_sb[:]))
-        nc.vector.tensor_copy(xe_picked[:, E_AT : E_AT + S], es_tab[:].indirect(coef_sb[:]))
-        place_scales(xe_planes, xe_picked)
+        nc.vector.tensor_copy(xv_picked[:, 0:S], xs_tab[:].indirect(offs_sb[:]))
+        nc.vector.tensor_copy(xv_picked[:, S : S + V], vs_tab[:].indirect(pts_sb[:]))
+        place_scales(xv_planes, xv_picked)
         ew_tab = placed.tile([P, W], I32, name="ew_tab", align_bytes=ALIGN, offset=EW_TAB_AT)
         load_words(ew_tab, e_words)
         xw = sb.tile([P, S], U32, name="xw", align_bytes=ALIGN)
         nc.vector.tensor_copy(xw[:], xw_tab[:].bitcast(U32).indirect(offs_sb[:]))
-        nc.vector.tensor_copy(v_picked[:], vs_tab[:].indirect(pts_sb[:]))
-        place_scales(v_plane, v_picked)
+        nc.vector.tensor_copy(e_picked[:], es_tab[:].indirect(coef_sb[:]))
+        place_scales(e_plane, e_picked)
         lift_sb = placed.tile([P, CHUNKS, V], F32, name="lift_sb", align_bytes=ALIGN, offset=LIFT_AT)
         for c in range(CHUNKS):
             nc.sync.dma_start(out=lift_sb[:, c, :], in_=lift[c * P : (c + 1) * P, :])
@@ -173,7 +172,7 @@ def tile_picked_ymionet_val_p_kernel(
         y_sb = placed.tile([P, CHUNKS, P, PACK], F32, name="y_sb", align_bytes=ALIGN, offset=Y_AT)
         for c in range(CHUNKS):
             bank = ps.tile([P, PACK, P], F32, name="y_bank%d" % c, tag="a%d" % c)
-            first_product(bank, w1_codes, w1_scales, xw[:, c * P : (c + 1) * P], xe_planes[:, X_AT + c * P : X_AT + (c + 1) * P])
+            first_product(bank, w1_codes, w1_scales, xw[:, c * P : (c + 1) * P], x_plane[:, c * P : (c + 1) * P])
             nc.scalar.copy(out=y_sb[:, c], in_=bank[:].rearrange("p r t -> p t r"))
 
         for start, stop in E_PIECES:
@@ -182,7 +181,7 @@ def tile_picked_ymionet_val_p_kernel(
         e_banks = []
         for c in range(CHUNKS):
             bank = ps.tile([P, PACK, P], F32, name="e_bank%d" % c, tag="b%d" % c)
-            first_product(bank, w2_codes, w2_scales, ew[:, c * P : (c + 1) * P], xe_planes[:, E_AT + c * P : E_AT + (c + 1) * P])
+            first_product(bank, w2_codes, w2_scales, ew[:, c * P : (c + 1) * P], e_plane[:, c * P : (c + 1) * P])
             e_banks.append(bank)
 
         z_bf = [sb.tile([P, P, PACK], BF16, name="z_bf%d" % c, align_bytes=ALIGN) for c in range(CHUNKS)]
@@ -240,7 +239,6 @@ def tile_picked_ymionet_val_p_kernel(
 
         def add_lift(c, src, blocks):
             nc.vector.tensor_tensor(result[c][:, cols(blocks)], src[:, cols(blocks)], lift_sb[:, c, cols(blocks)], ADD)
-            store(c, blocks)
 
         whole, left, right = range(POINT_BLOCKS), range(POINT_BLOCKS // 2), range(POINT_BLOCKS // 2, POINT_BLOCKS)
 
@@ -266,17 +264,25 @@ def tile_picked_ymionet_val_p_kernel(
         back_1r = turn_back(SECOND, right, "a2")
         make_z(LAST, late)
         add_lift(FIRST, back_0l, left)
+        store(FIRST, left)
         quantize_z(LAST)
         product_turned(LAST, left, "a3")
         product_turned(LAST, right, "b3")
         add_lift(FIRST, back_0r, right)
+        store(FIRST, right)
         back_2l = turn_back(THIRD, left, "b0")
         back_2r = turn_back(THIRD, right, "b1")
         add_lift(SECOND, back_1l, left)
+        store(SECOND, left)
         add_lift(SECOND, back_1r, right)
+        store(SECOND, right)
         back_3l = turn_back(LAST, left, "a0")
         back_3r = turn_back(LAST, right, "a1")
         add_lift(THIRD, back_2l, left)
+        store(THIRD, left)
         add_lift(THIRD, back_2r, right)
+        store(THIRD, right)
         add_lift(LAST, back_3l, left)
+        store(LAST, left)
         add_lift(LAST, back_3r, right)
+        store(LAST, right)

@@ -31,10 +31,11 @@ FIRST, SECOND, THIRD, LAST = range(CHUNKS)
 E_PIECES = ((0, P), (P, 2 * P), (2 * P, S))
 
 W2_AT = 0
-Y_AT = W2_AT
-W1_BF_AT = 8192
+PHI_ROW_AT = W2_AT
+Y_AT = PHI_ROW_AT + 1024
+W1_BF_AT = Y_AT + 8192
 VW_AT = W1_BF_AT
-EW_TAB_AT = 12288
+EW_TAB_AT = W1_BF_AT + 4096
 LIFT_AT = EW_TAB_AT + 8192
 VS_TAB_AT = EW_TAB_AT
 ES_TAB_AT = LIFT_AT
@@ -168,12 +169,19 @@ def tile_picked_ymionet_val_p_kernel(
             nc.tensor.transpose(col_bank[:, b, :], phi_pts[:, b * P : (b + 1) * P], ident[:])
         phi_col = sb.tile([P, POINT_BLOCKS], F32, name="phi_col")
         nc.scalar.copy(out=phi_col[:], in_=col_bank[:, :, 0])
+        half = V // 2
+        row_bank = ps.tile([P, POINT_BLOCKS // 2, P], F32, name="row_bank", tag="b3")
+        for b in range(POINT_BLOCKS // 2):
+            column = phi_col[:, POINT_BLOCKS // 2 + b : POINT_BLOCKS // 2 + b + 1]
+            nc.tensor.transpose(row_bank[:, b, :], column.to_broadcast([P, P]), ident[:])
 
         y_sb = placed.tile([P, CHUNKS, P, PACK], F32, name="y_sb", align_bytes=ALIGN, offset=Y_AT)
         for c in range(CHUNKS):
             bank = ps.tile([P, PACK, P], F32, name="y_bank%d" % c, tag="a%d" % c)
             first_product(bank, w1_codes, w1_scales, xw[:, c * P : (c + 1) * P], x_plane[:, c * P : (c + 1) * P])
             nc.scalar.copy(out=y_sb[:, c], in_=bank[:].rearrange("p r t -> p t r"))
+        phi_row = placed.tile([P, half], F32, name="phi_row", align_bytes=ALIGN, offset=PHI_ROW_AT)
+        nc.scalar.copy(out=phi_row[:], in_=row_bank[:].rearrange("p b t -> p (b t)"))
 
         for start, stop in E_PIECES:
             offsets = coef_sb[:, start // LIST_ROWS : stop // LIST_ROWS]
@@ -218,6 +226,24 @@ def tile_picked_ymionet_val_p_kernel(
             for b in blocks:
                 nc.scalar.activation(turned[c][:, b, :], bank[:, b, :], COPY, scale=phi_col[:, b : b + 1])
 
+        def product_plain(c, tag):
+            bank = ps.tile([P, half], F32, name="plain_bank%d" % c, tag=tag)
+            nc.tensor.matmul_mx(
+                out=bank[:],
+                lhsT=z_codes[c][:].bitcast(FP8X4),
+                lhsT_scale=z_scales[c][:],
+                rhs=vw[:, half:V].bitcast(FP8X4),
+                rhs_scale=v_plane[:, half:V],
+                start=True,
+                stop=True,
+            )
+            return bank
+
+        def scale_plain(c, bank):
+            scaled = sb.tile([P, V], F32, name="scaled%d" % c)
+            nc.vector.tensor_tensor(scaled[:, half:V], bank[:], phi_row[:], MULT)
+            return scaled
+
         def turn(bank, src, blocks, opens, closes):
             for b in blocks:
                 nc.tensor.matmul(
@@ -246,38 +272,38 @@ def tile_picked_ymionet_val_p_kernel(
         make_z(FIRST, slice(0, P))
         make_z(SECOND, early)
         quantize_z(FIRST)
+        plain_0 = product_plain(FIRST, "a1")
         product_turned(FIRST, left, "a0")
-        product_turned(FIRST, right, "a1")
         make_z(SECOND, late)
         make_z(THIRD, early)
         quantize_z(SECOND)
         back_0l = turn_back(FIRST, left, "b0")
         product_turned(SECOND, left, "a2")
         product_turned(SECOND, right, "a3")
-        back_0r = turn_back(FIRST, right, "b1")
         make_z(THIRD, late)
         make_z(LAST, early)
         quantize_z(THIRD)
         product_turned(THIRD, left, "a0")
-        product_turned(THIRD, right, "a1")
+        product_turned(THIRD, right, "b1")
         back_1l = turn_back(SECOND, left, "b2")
         back_1r = turn_back(SECOND, right, "a2")
         make_z(LAST, late)
-        add_lift(FIRST, back_0l, left)
-        store(FIRST, left)
+        back_0r = scale_plain(FIRST, plain_0)
         quantize_z(LAST)
         product_turned(LAST, left, "a3")
         product_turned(LAST, right, "b3")
+        add_lift(FIRST, back_0l, left)
+        store(FIRST, left)
         add_lift(FIRST, back_0r, right)
         store(FIRST, right)
-        back_2l = turn_back(THIRD, left, "b0")
-        back_2r = turn_back(THIRD, right, "b1")
+        back_2l = turn_back(THIRD, left, "a1")
+        back_2r = turn_back(THIRD, right, "b0")
         add_lift(SECOND, back_1l, left)
         store(SECOND, left)
         add_lift(SECOND, back_1r, right)
         store(SECOND, right)
         back_3l = turn_back(LAST, left, "a0")
-        back_3r = turn_back(LAST, right, "a1")
+        back_3r = turn_back(LAST, right, "b1")
         add_lift(THIRD, back_2l, left)
         store(THIRD, left)
         add_lift(THIRD, back_2r, right)

@@ -175,11 +175,11 @@ def tile_picked_ymionet_val_p_kernel(
             column = phi_col[:, POINT_BLOCKS // 2 + b : POINT_BLOCKS // 2 + b + 1]
             nc.tensor.transpose(row_bank[:, b, :], column.to_broadcast([P, P]), ident[:])
 
-        y_sb = placed.tile([P, CHUNKS, P, PACK], F32, name="y_sb", align_bytes=ALIGN, offset=Y_AT)
+        y_sb = placed.tile([P, CHUNKS, P // 2, PACK, 2], F32, name="y_sb", align_bytes=ALIGN, offset=Y_AT)
         for c in range(CHUNKS):
             bank = ps.tile([P, PACK, P], F32, name="y_bank%d" % c, tag="a%d" % c)
             first_product(bank, w1_codes, w1_scales, xw[:, c * P : (c + 1) * P], x_plane[:, c * P : (c + 1) * P])
-            nc.scalar.copy(out=y_sb[:, c], in_=bank[:].rearrange("p r t -> p t r"))
+            nc.scalar.copy(out=y_sb[:, c], in_=bank[:].rearrange("p r (a b) -> p a r b", b=2))
         phi_row = placed.tile([P, half], F32, name="phi_row", align_bytes=ALIGN, offset=PHI_ROW_AT)
         nc.scalar.copy(out=phi_row[:], in_=row_bank[:].rearrange("p b t -> p (b t)"))
 
@@ -202,8 +202,12 @@ def tile_picked_ymionet_val_p_kernel(
             return slice(blocks.start * P, blocks.stop * P)
 
         def make_z(c, entries):
+            pairs = slice(entries.start // 2, entries.stop // 2)
             nc.vector.tensor_tensor(
-                z_bf[c][:, entries, :], e_banks[c][:].rearrange("p r t -> p t r")[:, entries, :], y_sb[:, c, entries, :], MULT
+                z_bf[c][:].rearrange("p (a b) r -> p a r b", b=2)[:, pairs],
+                e_banks[c][:].rearrange("p r (a b) -> p a r b", b=2)[:, pairs],
+                y_sb[:, c, pairs],
+                MULT,
             )
 
         def quantize_z(c):

@@ -21,6 +21,7 @@ P = 128
 PACK = 4
 QUADRANT = 32
 SPREAD = 8
+X_ROW = 4
 LIST_ROWS = 16
 CHUNKS = S // P
 POINT_BLOCKS = V // P
@@ -28,6 +29,7 @@ ALIGN = 64
 
 FIRST, SECOND, THIRD, LAST = range(CHUNKS)
 
+V_PLACES = 48
 E_PIECES = ((0, P), (P, 2 * P), (2 * P, S))
 
 W2_AT = 0
@@ -37,7 +39,8 @@ W1_BF_AT = Y_AT + 8192
 VW_AT = W1_BF_AT
 EW_TAB_AT = W1_BF_AT + 4096
 LIFT_AT = EW_TAB_AT + 8192
-VS_TAB_AT = EW_TAB_AT
+W1_AT = LIFT_AT + 8192
+XS_TAB_AT = EW_TAB_AT
 ES_TAB_AT = LIFT_AT
 
 
@@ -65,10 +68,10 @@ def tile_picked_ymionet_val_p_kernel(
         def load_weight(tile, w):
             nc.sync.dma_start(out=tile[:], in_=w.rearrange("(p j) c -> p j c", j=PACK))
 
-        def place_scales(planes, picked):
+        def place_scales(planes, picked, row):
             for r in range(4):
                 nc.sync.dma_start(
-                    out=planes[r:P:QUADRANT, :].bitcast(I32), in_=picked[SPREAD * r : P : QUADRANT, :].bitcast(I32)
+                    out=planes[row + r : P : QUADRANT, :].bitcast(I32), in_=picked[SPREAD * r : P : QUADRANT, :].bitcast(I32)
                 )
 
         def cast_views(grouped, raw, places, tiles):
@@ -77,30 +80,31 @@ def tile_picked_ymionet_val_p_kernel(
                 raw[:].rearrange("p j (m r) -> p m j r", r=PACK)[:, places, :, tiles],
             )
 
-        xs_tab = sb.tile([P, T], U8, name="xs_tab", align_bytes=ALIGN)
-        vs_tab = placed.tile([P, G], U8, name="vs_tab", align_bytes=ALIGN, offset=VS_TAB_AT)
+        xs_tab = placed.tile([P, T], U8, name="xs_tab", align_bytes=ALIGN, offset=XS_TAB_AT)
+        vs_tab = sb.tile([P, G], U8, name="vs_tab", align_bytes=ALIGN)
         es_tab = placed.tile([P, W], U8, name="es_tab", align_bytes=ALIGN, offset=ES_TAB_AT)
         xw_tab = sb.tile([P, T], I32, name="xw_tab", align_bytes=ALIGN)
         vw_tab = sb.tile([P, G], I32, name="vw_tab", align_bytes=ALIGN)
         phi_tab = sb.tile([P, G], F32, name="phi_tab")
-        xv_picked = sb.tile([P, S + V], U8, name="xv_picked", align_bytes=ALIGN)
-        xv_planes = sb.tile([P, S + V], U8, name="xv_planes", align_bytes=ALIGN)
-        e_picked = sb.tile([P, S], U8, name="e_picked", align_bytes=ALIGN)
-        e_plane = sb.tile([P, S], U8, name="e_plane", align_bytes=ALIGN)
-        x_plane, v_plane = xv_planes[:, 0:S], xv_planes[:, S : S + V]
+        x_picked = sb.tile([P, S], U8, name="x_picked", align_bytes=ALIGN)
+        x_rows = sb.tile([P, S], U8, name="x_rows", align_bytes=ALIGN)
+        ev_picked = sb.tile([P, S + V], U8, name="ev_picked", align_bytes=ALIGN)
+        ev_planes = sb.tile([P, S + V], U8, name="ev_planes", align_bytes=ALIGN)
+        x_plane = x_rows[X_ROW:P, :]
+        e_plane, v_plane = ev_planes[:, 0:S], ev_planes[:, S : S + V]
 
-        nc.vector.memset(phi_tab[:], 0.0)
-        for tile in (xs_tab, vs_tab, es_tab, xv_planes, e_plane):
+        for tile in (xs_tab, vs_tab, es_tab, x_rows, ev_planes):
             nc.vector.memset(tile[:].bitcast(I32), 0)
+        nc.vector.memset(phi_tab[0 : P - 1, :], 0.0)
 
         load_words(xw_tab, x_words)
         offs_sb = load_list("offs_sb", offs)
         pts_sb = load_list("pts_sb", pts)
         coef_sb = load_list("coef_sb", coef)
-        nc.sync.dma_start(out=phi_tab[0:1, :], in_=phi[0:1, :])
+        nc.sync.dma_start(out=phi_tab[P - 1 : P, :], in_=phi[0:1, :])
         load_scales(xs_tab, x_scales)
         load_scales(vs_tab, v_scales)
-        w1_raw = sb.tile([P, PACK, H], F32, name="w1_raw", align_bytes=ALIGN)
+        w1_raw = placed.tile([P, PACK, H], F32, name="w1_raw", align_bytes=ALIGN, offset=W1_AT)
         load_weight(w1_raw, w1)
         load_scales(es_tab, e_scales)
         w2_raw = placed.tile([P, PACK, H], F32, name="w2_raw", align_bytes=ALIGN, offset=W2_AT)
@@ -113,15 +117,15 @@ def tile_picked_ymionet_val_p_kernel(
         nc.scalar.copy(out=ident[:], in_=zero[:].to_broadcast([P, P]))
         make_identity(nc, ident[:], nomemset=True)
 
-        nc.vector.tensor_copy(xv_picked[:, 0:S], xs_tab[:].indirect(offs_sb[:]))
-        nc.vector.tensor_copy(xv_picked[:, S : S + V], vs_tab[:].indirect(pts_sb[:]))
-        place_scales(xv_planes, xv_picked)
+        nc.vector.tensor_copy(x_picked[:], xs_tab[:].indirect(offs_sb[:]))
+        place_scales(x_rows, x_picked, X_ROW)
         ew_tab = placed.tile([P, W], I32, name="ew_tab", align_bytes=ALIGN, offset=EW_TAB_AT)
         load_words(ew_tab, e_words)
         xw = sb.tile([P, S], U32, name="xw", align_bytes=ALIGN)
         nc.vector.tensor_copy(xw[:], xw_tab[:].bitcast(U32).indirect(offs_sb[:]))
-        nc.vector.tensor_copy(e_picked[:], es_tab[:].indirect(coef_sb[:]))
-        place_scales(e_plane, e_picked)
+        nc.vector.tensor_copy(ev_picked[:, S : S + V], vs_tab[:].indirect(pts_sb[:]))
+        nc.vector.tensor_copy(ev_picked[:, 0:S], es_tab[:].indirect(coef_sb[:]))
+        place_scales(ev_planes, ev_picked, 0)
         lift_sb = placed.tile([P, CHUNKS, V], F32, name="lift_sb", align_bytes=ALIGN, offset=LIFT_AT)
         for c in range(CHUNKS):
             nc.sync.dma_start(out=lift_sb[:, c, :], in_=lift[c * P : (c + 1) * P, :])
@@ -138,9 +142,9 @@ def tile_picked_ymionet_val_p_kernel(
 
         nc.scalar.activation(phi_pts[:], phi_tab[:].indirect(pts_sb[:]), COPY)
         nc.scalar.copy(*cast_views(w1_bf, w1_raw, slice(0, P), slice(0, PACK)))
-        nc.vector.tensor_copy(*cast_views(w2_bf, w2_raw, slice(0, P // 2), slice(2, PACK)))
+        nc.vector.tensor_copy(*cast_views(w2_bf, w2_raw, slice(0, V_PLACES), slice(2, PACK)))
         nc.scalar.copy(*cast_views(w2_bf, w2_raw, slice(0, P), slice(0, 2)))
-        nc.scalar.copy(*cast_views(w2_bf, w2_raw, slice(P // 2, P), slice(2, PACK)))
+        nc.scalar.copy(*cast_views(w2_bf, w2_raw, slice(V_PLACES, P), slice(2, PACK)))
         nc.vector.quantize_mx(out=w1_codes[:].bitcast(FP8X4), scales=w1_scales[:], in_=w1_bf[:])
         nc.vector.tensor_copy(vw[:], vw_tab[:].bitcast(U32).indirect(pts_sb[:]))
         for h in range(2):
@@ -167,8 +171,8 @@ def tile_picked_ymionet_val_p_kernel(
         col_bank = ps.tile([P, POINT_BLOCKS, P], F32, name="col_bank", tag="b2")
         for b in range(POINT_BLOCKS):
             nc.tensor.transpose(col_bank[:, b, :], phi_pts[:, b * P : (b + 1) * P], ident[:])
-        phi_col = sb.tile([P, POINT_BLOCKS], F32, name="phi_col")
-        nc.scalar.copy(out=phi_col[:], in_=col_bank[:, :, 0])
+        phi_col = placed.tile([P, POINT_BLOCKS], F32, name="phi_col", align_bytes=ALIGN, offset=W1_AT)
+        nc.scalar.copy(out=phi_col[:], in_=col_bank[:, :, P - 1])
         half = V // 2
         row_bank = ps.tile([P, POINT_BLOCKS // 2, P], F32, name="row_bank", tag="b3")
         for b in range(POINT_BLOCKS // 2):

@@ -25,7 +25,7 @@ X_ROW = 4
 LIST_ROWS = 16
 CHUNKS = S // P
 POINT_BLOCKS = V // P
-ALIGN = 64
+ALIGN = 256
 
 FIRST, SECOND, THIRD, LAST = range(CHUNKS)
 
@@ -85,7 +85,7 @@ def tile_picked_ymionet_val_p_kernel(
         es_tab = placed.tile([P, W], U8, name="es_tab", align_bytes=ALIGN, offset=ES_TAB_AT)
         xw_tab = sb.tile([P, T], I32, name="xw_tab", align_bytes=ALIGN)
         vw_tab = sb.tile([P, G], I32, name="vw_tab", align_bytes=ALIGN)
-        phi_tab = sb.tile([P, G], F32, name="phi_tab")
+        phi_tab = sb.tile([P, G], F32, name="phi_tab", align_bytes=ALIGN)
         x_picked = sb.tile([P, S], U8, name="x_picked", align_bytes=ALIGN)
         x_rows = sb.tile([P, S], U8, name="x_rows", align_bytes=ALIGN)
         ev_picked = sb.tile([P, S + V], U8, name="ev_picked", align_bytes=ALIGN)
@@ -200,7 +200,7 @@ def tile_picked_ymionet_val_p_kernel(
         z_codes = [sb.tile([P, P], U32, name="z_codes%d" % c, align_bytes=ALIGN) for c in range(CHUNKS)]
         z_scales = [sb.tile([P, P], U8, name="z_scales%d" % c, align_bytes=ALIGN) for c in range(CHUNKS)]
         turned = [sb.tile([P, POINT_BLOCKS, P], F32, name="turned%d" % c) for c in range(CHUNKS)]
-        result = [sb.tile([P, V], F32, name="result%d" % c) for c in range(CHUNKS)]
+        result = [sb.tile([P, V], F32, name="result%d" % c, align_bytes=ALIGN) for c in range(CHUNKS)]
 
         def cols(blocks):
             return slice(blocks.start * P, blocks.stop * P)

from contextlib import ExitStack

import concourse.mybir as mybir
from concourse.masks import make_identity

K, T, S, H, V, W, G = 512, 1024, 512, 512, 512, 2048, 1024
FLOPS = 2 * K * H * S * 2 + 2 * H * S * V

F32 = mybir.dt.float32
BF16 = mybir.dt.bfloat16
I32 = mybir.dt.int32
U32 = mybir.dt.uint32
U16 = mybir.dt.uint16
U8 = mybir.dt.uint8
FP8X4 = mybir.dt.float8_e4m3fn_x4
MULT = mybir.AluOpType.mult
ADD = mybir.AluOpType.add
COPY = mybir.ActivationFunctionType.Copy

P = 128
PACK = 4
QUADRANT = 32
SPREAD = 8
X_ROW = 4
LIST_ROWS = 16
CHUNKS = S // P
POINT_BLOCKS = V // P
ALIGN = 256

FIRST, SECOND, THIRD, LAST = range(CHUNKS)

V_PLACES = 48
E_PIECES = ((0, P), (P, 2 * P), (2 * P, S))

W2_AT = 0
PHI_ROW_AT = W2_AT
Y_AT = PHI_ROW_AT + 1024
W1_BF_AT = Y_AT + 8192
VW_AT = W1_BF_AT
EW_TAB_AT = W1_BF_AT + 4096
LIFT_AT = EW_TAB_AT + 8192
W1_AT = LIFT_AT + 8192
XS_TAB_AT = EW_TAB_AT
ES_TAB_AT = LIFT_AT


def tile_picked_ymionet_val_p_kernel(
    tc, x_words, x_scales, e_words, e_scales, w1, w2, v_words, v_scales, phi, lift, offs, coef, pts, out
):
    nc = tc.nc
    with ExitStack() as ctx:
        lists = ctx.enter_context(tc.tile_pool(name="lists", bufs=1))
        sb = ctx.enter_context(tc.tile_pool(name="sb", bufs=1))
        placed = ctx.enter_context(tc.tile_pool(name="placed", bufs=1))
        ps = ctx.enter_context(tc.psum_pool(name="ps", bufs=1))

        def load_scales(tile, scales):
            nc.sync.dma_start(out=tile[0:P:SPREAD, :].bitcast(I32), in_=scales[0].bitcast(I32))

        def load_list(name, src):
            tile = lists.tile([P, S // LIST_ROWS], U16, name=name)
            nc.sync.dma_start(tile[:], src)
            return tile

        def load_words(tile, words):
            nc.sync.dma_start(out=tile[:], in_=words[0].rearrange("p n t -> p (n t)").bitcast(I32))

        def load_weight(tile, w):
            nc.sync.dma_start(out=tile[:], in_=w.rearrange("(p j) c -> p j c", j=PACK))

        def place_scales(planes, picked, row):
            for r in range(4):
                nc.sync.dma_start(
                    out=planes[row + r : P : QUADRANT, :].bitcast(I32), in_=picked[SPREAD * r : P : QUADRANT, :].bitcast(I32)
                )

        def cast_views(grouped, raw, places, tiles):
            return (
                grouped[:].rearrange("p (r m j) -> p m j r", r=PACK, j=PACK)[:, places, :, tiles],
                raw[:].rearrange("p j (m r) -> p m j r", r=PACK)[:, places, :, tiles],
            )

        xs_tab = placed.tile([P, T], U8, name="xs_tab", align_bytes=ALIGN, offset=XS_TAB_AT)
        vs_tab = sb.tile([P, G], U8, name="vs_tab", align_bytes=ALIGN)
        es_tab = placed.tile([P, W], U8, name="es_tab", align_bytes=ALIGN, offset=ES_TAB_AT)
        xw_tab = sb.tile([P, T], I32, name="xw_tab", align_bytes=ALIGN)
        vw_tab = sb.tile([P, G], I32, name="vw_tab", align_bytes=ALIGN)
        phi_tab = sb.tile([P, G], F32, name="phi_tab", align_bytes=ALIGN)
        x_picked = sb.tile([P, S], U8, name="x_picked", align_bytes=ALIGN)
        x_rows = sb.tile([P, S], U8, name="x_rows", align_bytes=ALIGN)
        ev_picked = sb.tile([P, S + V], U8, name="ev_picked", align_bytes=ALIGN)
        ev_planes = sb.tile([P, S + V], U8, name="ev_planes", align_bytes=ALIGN)
        x_plane = x_rows[X_ROW:P, :]
        e_plane, v_plane = ev_planes[:, 0:S], ev_planes[:, S : S + V]

        for tile in (xs_tab, vs_tab, es_tab, x_rows, ev_planes):
            nc.vector.memset(tile[:].bitcast(I32), 0)
        nc.vector.memset(phi_tab[0 : P - 1, :], 0.0)

        load_words(xw_tab, x_words)
        offs_sb = load_list("offs_sb", offs)
        pts_sb = load_list("pts_sb", pts)
        coef_sb = load_list("coef_sb", coef)
        nc.sync.dma_start(out=phi_tab[P - 1 : P, :], in_=phi[0:1, :])
        load_scales(xs_tab, x_scales)
        load_scales(vs_tab, v_scales)
        w1_raw = placed.tile([P, PACK, H], F32, name="w1_raw", align_bytes=ALIGN, offset=W1_AT)
        load_weight(w1_raw, w1)
        load_scales(es_tab, e_scales)
        w2_raw = placed.tile([P, PACK, H], F32, name="w2_raw", align_bytes=ALIGN, offset=W2_AT)
        load_weight(w2_raw, w2)
        load_words(vw_tab, v_words)

        ident = sb.tile([P, P], F32, name="ident")
        zero = sb.tile([P, 1], F32, name="zero")
        nc.gpsimd.memset(zero[:], 0.0)
        nc.scalar.copy(out=ident[:], in_=zero[:].to_broadcast([P, P]))
        make_identity(nc, ident[:], nomemset=True)

        nc.vector.tensor_copy(x_picked[:], xs_tab[:].indirect(offs_sb[:]))
        place_scales(x_rows, x_picked, X_ROW)
        ew_tab = placed.tile([P, W], I32, name="ew_tab", align_bytes=ALIGN, offset=EW_TAB_AT)
        load_words(ew_tab, e_words)
        xw = sb.tile([P, S], U32, name="xw", align_bytes=ALIGN)
        nc.vector.tensor_copy(xw[:], xw_tab[:].bitcast(U32).indirect(offs_sb[:]))
        nc.vector.tensor_copy(ev_picked[:, S : S + V], vs_tab[:].indirect(pts_sb[:]))
        nc.vector.tensor_copy(ev_picked[:, 0:S], es_tab[:].indirect(coef_sb[:]))
        place_scales(ev_planes, ev_picked, 0)
        lift_sb = placed.tile([P, CHUNKS, V], F32, name="lift_sb", align_bytes=ALIGN, offset=LIFT_AT)
        for c in range(CHUNKS):
            nc.sync.dma_start(out=lift_sb[:, c, :], in_=lift[c * P : (c + 1) * P, :])

        phi_pts = sb.tile([P, V], F32, name="phi_pts")
        w1_bf = placed.tile([P, H * PACK], BF16, name="w1_bf", align_bytes=ALIGN, offset=W1_BF_AT)
        w2_bf = sb.tile([P, H * PACK], BF16, name="w2_bf", align_bytes=ALIGN)
        w1_codes = sb.tile([P, H], U32, name="w1_codes", align_bytes=ALIGN)
        w2_codes = sb.tile([P, H], U32, name="w2_codes", align_bytes=ALIGN)
        vw = placed.tile([P, V], U32, name="vw", align_bytes=ALIGN, offset=VW_AT)
        ew = sb.tile([P, S], U32, name="ew", align_bytes=ALIGN)
        w1_scales = sb.tile([P, H], U8, name="w1_scales", align_bytes=ALIGN)
        w2_scales = sb.tile([P, H], U8, name="w2_scales", align_bytes=ALIGN)

        nc.scalar.activation(phi_pts[:], phi_tab[:].indirect(pts_sb[:]), COPY)
        nc.scalar.copy(*cast_views(w1_bf, w1_raw, slice(0, P), slice(0, PACK)))
        nc.vector.tensor_copy(*cast_views(w2_bf, w2_raw, slice(0, V_PLACES), slice(2, PACK)))
        nc.scalar.copy(*cast_views(w2_bf, w2_raw, slice(0, P), slice(0, 2)))
        nc.scalar.copy(*cast_views(w2_bf, w2_raw, slice(V_PLACES, P), slice(2, PACK)))
        nc.vector.quantize_mx(out=w1_codes[:].bitcast(FP8X4), scales=w1_scales[:], in_=w1_bf[:])
        nc.vector.tensor_copy(vw[:], vw_tab[:].bitcast(U32).indirect(pts_sb[:]))
        for h in range(2):
            places = slice(h * H // 2, (h + 1) * H // 2)
            nc.vector.quantize_mx(
                out=w2_codes[:, places].bitcast(FP8X4),
                scales=w2_scales[:, places],
                in_=w2_bf[:, 2 * h * H : 2 * (h + 1) * H],
            )

        def first_product(bank, codes, scales, words, word_scales):
            for r in range(PACK):
                hid = slice(r * P, (r + 1) * P)
                nc.tensor.matmul_mx(
                    out=bank[:, r, :],
                    lhsT=codes[:, hid].bitcast(FP8X4),
                    lhsT_scale=scales[:, hid],
                    rhs=words.bitcast(FP8X4),
                    rhs_scale=word_scales,
                    start=True,
                    stop=True,
                )

        col_bank = ps.tile([P, POINT_BLOCKS, P], F32, name="col_bank", tag="b2")
        for b in range(POINT_BLOCKS):
            nc.tensor.transpose(col_bank[:, b, :], phi_pts[:, b * P : (b + 1) * P], ident[:])
        phi_col = placed.tile([P, POINT_BLOCKS], F32, name="phi_col", align_bytes=ALIGN, offset=W1_AT)
        nc.scalar.copy(out=phi_col[:], in_=col_bank[:, :, P - 1])
        half = V // 2
        row_bank = ps.tile([P, POINT_BLOCKS // 2, P], F32, name="row_bank", tag="b3")
        for b in range(POINT_BLOCKS // 2):
            column = phi_col[:, POINT_BLOCKS // 2 + b : POINT_BLOCKS // 2 + b + 1]
            nc.tensor.transpose(row_bank[:, b, :], column.to_broadcast([P, P]), ident[:])

        y_sb = placed.tile([P, CHUNKS, P // 2, PACK, 2], F32, name="y_sb", align_bytes=ALIGN, offset=Y_AT)
        for c in range(CHUNKS):
            bank = ps.tile([P, PACK, P], F32, name="y_bank%d" % c, tag="a%d" % c)
            first_product(bank, w1_codes, w1_scales, xw[:, c * P : (c + 1) * P], x_plane[:, c * P : (c + 1) * P])
            nc.scalar.copy(out=y_sb[:, c], in_=bank[:].rearrange("p r (a b) -> p a r b", b=2))
        phi_row = placed.tile([P, half], F32, name="phi_row", align_bytes=ALIGN, offset=PHI_ROW_AT)
        nc.scalar.copy(out=phi_row[:], in_=row_bank[:].rearrange("p b t -> p (b t)"))

        for start, stop in E_PIECES:
            offsets = coef_sb[:, start // LIST_ROWS : stop // LIST_ROWS]
            nc.vector.tensor_copy(ew[:, start:stop], ew_tab[:].bitcast(U32).indirect(offsets))
        e_banks = []
        for c in range(CHUNKS):
            bank = ps.tile([P, PACK, P], F32, name="e_bank%d" % c, tag="b%d" % c)
            first_product(bank, w2_codes, w2_scales, ew[:, c * P : (c + 1) * P], e_plane[:, c * P : (c + 1) * P])
            e_banks.append(bank)

        z_bf = [sb.tile([P, P, PACK], BF16, name="z_bf%d" % c, align_bytes=ALIGN) for c in range(CHUNKS)]
        z_codes = [sb.tile([P, P], U32, name="z_codes%d" % c, align_bytes=ALIGN) for c in range(CHUNKS)]
        z_scales = [sb.tile([P, P], U8, name="z_scales%d" % c, align_bytes=ALIGN) for c in range(CHUNKS)]
        turned = [sb.tile([P, POINT_BLOCKS, P], F32, name="turned%d" % c) for c in range(CHUNKS)]
        result = [sb.tile([P, V], F32, name="result%d" % c, align_bytes=ALIGN) for c in range(CHUNKS)]

        def cols(blocks):
            return slice(blocks.start * P, blocks.stop * P)

        def make_z(c, entries):
            pairs = slice(entries.start // 2, entries.stop // 2)
            nc.vector.tensor_tensor(
                z_bf[c][:].rearrange("p (a b) r -> p a r b", b=2)[:, pairs],
                e_banks[c][:].rearrange("p r (a b) -> p a r b", b=2)[:, pairs],
                y_sb[:, c, pairs],
                MULT,
            )

        def quantize_z(c):
            nc.vector.quantize_mx(
                out=z_codes[c][:].bitcast(FP8X4), scales=z_scales[c][:], in_=z_bf[c][:].rearrange("p t r -> p (t r)")
            )

        def product_turned(c, blocks, tag):
            bank = ps.tile([P, POINT_BLOCKS, P], F32, name="turned_bank%d_%d" % (c, blocks.start), tag=tag)
            for b in blocks:
                nc.tensor.matmul_mx(
                    out=bank[:, b, :],
                    lhsT=vw[:, b * P : (b + 1) * P].bitcast(FP8X4),
                    lhsT_scale=v_plane[:, b * P : (b + 1) * P],
                    rhs=z_codes[c][:].bitcast(FP8X4),
                    rhs_scale=z_scales[c][:],
                    start=True,
                    stop=True,
                )
            for b in blocks:
                nc.scalar.activation(turned[c][:, b, :], bank[:, b, :], COPY, scale=phi_col[:, b : b + 1])

        def product_plain(c, tag):
            bank = ps.tile([P, half], F32, name="plain_bank%d" % c, tag=tag)
            nc.tensor.matmul_mx(
                out=bank[:],
                lhsT=z_codes[c][:].bitcast(FP8X4),
                lhsT_scale=z_scales[c][:],
                rhs=vw[:, half:V].bitcast(FP8X4),
                rhs_scale=v_plane[:, half:V],
                start=True,
                stop=True,
            )
            return bank

        def scale_plain(c, bank):
            scaled = sb.tile([P, V], F32, name="scaled%d" % c)
            nc.vector.tensor_tensor(scaled[:, half:V], bank[:], phi_row[:], MULT)
            return scaled

        def turn(bank, src, blocks, opens, closes):
            for b in blocks:
                nc.tensor.matmul(
                    bank[:, b * P : (b + 1) * P],
                    src[:, b, :],
                    ident[:],
                    start=opens and b == blocks[0],
                    stop=closes and b == blocks[-1],
                    is_transpose=True,
                )

        def turn_back(c, blocks, tag):
            bank = ps.tile([P, V], F32, name="back_bank%d_%d" % (c, blocks.start), tag=tag)
            turn(bank, turned[c], blocks, True, True)
            return bank

        def store(c, blocks):
            nc.sync.dma_start(out=out[c * P : (c + 1) * P, cols(blocks)], in_=result[c][:, cols(blocks)])

        def add_lift(c, src, blocks):
            nc.vector.tensor_tensor(result[c][:, cols(blocks)], src[:, cols(blocks)], lift_sb[:, c, cols(blocks)], ADD)

        whole, left, right = range(POINT_BLOCKS), range(POINT_BLOCKS // 2), range(POINT_BLOCKS // 2, POINT_BLOCKS)

        early, late = slice(0, P // 2), slice(P // 2, P)
        make_z(FIRST, slice(0, P))
        make_z(SECOND, early)
        quantize_z(FIRST)
        plain_0 = product_plain(FIRST, "a1")
        product_turned(FIRST, left, "a0")
        make_z(SECOND, late)
        make_z(THIRD, early)
        quantize_z(SECOND)
        back_0l = turn_back(FIRST, left, "b0")
        product_turned(SECOND, left, "a2")
        product_turned(SECOND, right, "a3")
        make_z(THIRD, late)
        make_z(LAST, early)
        quantize_z(THIRD)
        product_turned(THIRD, left, "a0")
        product_turned(THIRD, right, "b1")
        back_1l = turn_back(SECOND, left, "b2")
        back_1r = turn_back(SECOND, right, "a2")
        make_z(LAST, late)
        back_0r = scale_plain(FIRST, plain_0)
        quantize_z(LAST)
        product_turned(LAST, left, "a3")
        product_turned(LAST, right, "b3")
        add_lift(FIRST, back_0l, left)
        store(FIRST, left)
        add_lift(FIRST, back_0r, right)
        store(FIRST, right)
        back_2l = turn_back(THIRD, left, "a1")
        back_2r = turn_back(THIRD, right, "b0")
        add_lift(SECOND, back_1l, left)
        store(SECOND, left)
        add_lift(SECOND, back_1r, right)
        store(SECOND, right)
        back_3l = turn_back(LAST, left, "a0")
        back_3r = turn_back(LAST, right, "b1")
        add_lift(THIRD, back_2l, left)
        store(THIRD, left)
        add_lift(THIRD, back_2r, right)
        store(THIRD, right)
        add_lift(LAST, back_3l, left)
        store(LAST, left)
        add_lift(LAST, back_3r, right)
        store(LAST, right)
